import numpy as np
import ml_dtypes


def mxq(x, axis, fmt="e4m3"):
    dtype, down = {"e4m3": (ml_dtypes.float8_e4m3fn, 7), "e5m2": (ml_dtypes.float8_e5m2, 14)}[fmt]
    v = np.moveaxis(np.asarray(x, np.float32).astype(ml_dtypes.bfloat16).astype(np.float64), axis, -1)
    blocks = v.reshape(v.shape[:-1] + (-1, 32))
    amax = np.abs(blocks).max(-1, keepdims=True)
    byte = np.maximum(np.where(amax > 0, np.frexp(amax)[1] - 1 + 127, 0) - down, 1)
    scale = np.exp2(byte - 127.0)
    codes = (blocks / scale).astype(np.float32).astype(dtype).astype(np.float64)
    return np.moveaxis((codes * scale).reshape(v.shape), -1, axis)


WIDE = False


def mx_kscale(k):
    if not WIDE:
        return np.ones(k)
    levels = np.array([10, -10, 5, -5, 0])
    if k % 512:
        return np.exp2(np.random.permutation(np.resize(levels, k // 32))).repeat(32)
    a = np.empty((k // 512, 16))
    for p in range(k // 512):
        a[p, :8] = np.random.permutation(np.resize(levels, 8))
        for g in range(8):
            far = levels[np.abs(levels - a[p, g]) >= 10]
            a[p, g + 8] = far[np.random.randint(len(far))]
    return np.exp2(a.ravel()).repeat(32)


def f64(x):
    return np.asarray(x).astype(np.float64)


def striped(idx):
    return np.tile(idx.reshape(-1, 16).T, (8, 1)).astype(np.uint16)


def unstriped(offs):
    return offs[:16].T.reshape(-1).astype(np.int64)


def pack_weight(w):
    k, n = w.shape
    w = f64(np.asarray(w, np.float32).astype(ml_dtypes.bfloat16)).reshape(k // 32, 32, n)
    amax = np.abs(w).max(1)
    byte = np.clip(np.where(amax > 0, np.frexp(amax)[1] - 1 + 127 - 7, 1), 1, 254)
    scaled = (w * np.exp2(127.0 - byte)[:, None, :]).reshape(k, n).astype(np.float32)
    words = np.ascontiguousarray(scaled.reshape(k // 512, 128, 4, n).transpose(0, 1, 3, 2)).astype(ml_dtypes.float8_e4m3fn).view(np.uint8)
    return words, np.ascontiguousarray(byte.astype(np.uint8).reshape(k // 512, 16, n))


def unpack_weight(words, scales):
    g, p, n, _ = words.shape
    vals = np.ascontiguousarray(words).view(ml_dtypes.float8_e4m3fn).astype(np.float64) * np.repeat(np.exp2(scales.astype(np.float64) - 127.0), 8, axis=1)[..., None]
    return vals.transpose(0, 1, 3, 2).reshape(g * 512, n)


E2M1 = np.array([0.0, 0.5, 1.0, 1.5, 2.0, 3.0, 4.0, 6.0, -0.0, -0.5, -1.0, -1.5, -2.0, -3.0, -4.0, -6.0])


def pack_fp4(w):
    k, n = w.shape
    w = f64(np.asarray(w, np.float32).astype(ml_dtypes.bfloat16)).reshape(k // 32, 32, n)
    amax = np.abs(w).max(1)
    mant, ex = np.frexp(amax / 6.0)
    byte = np.clip(np.where(amax > 0, np.where(mant > 0.5, ex, ex - 1) + 127, 1), 1, 254)
    scaled = (w * np.exp2(127.0 - byte)[:, None, :]).reshape(k, n).astype(np.float32)
    c = np.ascontiguousarray(scaled.reshape(k // 512, 128, 4, n).transpose(0, 1, 3, 2)).astype(ml_dtypes.float4_e2m1fn).view(np.uint8) & 0xF
    words = (c[..., 0::2] | (c[..., 1::2] << 4)).reshape(k // 512, 128, 2 * n)
    return np.ascontiguousarray(words), np.ascontiguousarray(byte.astype(np.uint8).reshape(k // 512, 16, n))


def unpack_fp4(words, scales):
    g, _, n = scales.shape
    words = np.ascontiguousarray(words).reshape(g, 128, n, 2)
    nib = np.empty((g, 128, n, 4), np.uint8)
    nib[..., 0::2] = words & 0xF
    nib[..., 1::2] = words >> 4
    vals = E2M1[nib] * np.repeat(np.exp2(scales.astype(np.float64) - 127.0), 8, axis=1)[..., None]
    return vals.transpose(0, 1, 3, 2).reshape(g * 512, n)


def planes(y):
    n, m = y.shape
    v = y.astype(np.float32).astype(ml_dtypes.bfloat16).astype(np.float64).reshape(n // 32, 32, m)
    top = np.abs(v).max(1)
    byte = np.clip(np.where(top > 0, np.frexp(top)[1] - 1 + 127 - 7, 1), 1, 254)
    codes = (v * np.exp2(127.0 - byte)[:, None, :]).reshape(n, m).astype(np.float32).astype(ml_dtypes.float8_e4m3fn).view(np.uint8)
    words = codes.reshape(n // 512, 128, 4, m).transpose(0, 1, 3, 2)
    return np.ascontiguousarray(words), np.ascontiguousarray(byte.astype(np.uint8).reshape(n // 512, 16, m))


K, T, S, V, H = 512, 2048, 512, 512, 512


def setup_inputs():
    n = np.random.standard_normal
    s = mx_kscale(K)[:, None]
    u = mx_kscale(S)
    packed_xT = pack_weight(n((K, T)) * s)
    packed_w1 = pack_fp4(n((K, H)) / np.sqrt(K) / s)
    return {
        "x_words": packed_xT[0],
        "x_scales": packed_xT[1],
        "wa": (n((K, H)) / np.sqrt(K) / s).astype(np.float32),
        "wb": (n((K, H)) / np.sqrt(K) / s).astype(np.float32),
        "gt": (np.random.uniform(0.5, 1.5, (S, 1)) * u[:, None]).astype(np.float32),
        "gi": (np.random.uniform(0.5, 1.5, (S, 1)) / u[:, None]).astype(np.float32),
        "w1_words": packed_w1[0],
        "w1_scales": packed_w1[1],
        "gk": (np.random.uniform(0.5, 1.5, (H, 1)) * u[:, None]).astype(np.float32),
        "gq": (np.random.uniform(0.5, 1.5, (H, 1)) / u[:, None]).astype(np.float32),
        "res": (2 * n((H, V))).astype(np.float32),
        "offs": striped(np.random.permutation(T)[:S]),
        "qs": striped(np.random.permutation(T)[:V]),
    }


def reference(x_words, x_scales, wa, wb, gt, gi, w1_words, w1_scales, gk, gq, res, offs, qs):
    xq = unpack_weight(x_words, x_scales)[:, unstriped(offs)]
    a = xq.T @ mxq(f64(wa), 0, "e4m3")
    z = f64(gt) * a
    b = xq.T @ mxq(f64(wb), 0, "e4m3")
    z2 = f64(gi) * b
    cv = 0.0625 * ((mxq(z, 0, "e4m3").T @ mxq(z2, 0, "e4m3")))
    z3 = f64(gk) * cv
    x_qs = unpack_weight(x_words, x_scales)[:, unstriped(qs)]
    y = unpack_fp4(w1_words, w1_scales).T @ x_qs
    z4 = f64(gq) * y
    out_0 = f64(res) - (0.03125 * ((mxq(z3, 0, "e4m3").T @ mxq(z4, 0, "e4m3"))))
    return (out_0,) + planes(out_0)

@@ -1,0 +1,235 @@
+from contextlib import ExitStack
+
+import concourse.mybir as mybir
+from concourse.masks import make_identity
+
+F32 = mybir.dt.float32
+BF16 = mybir.dt.bfloat16
+I32 = mybir.dt.int32
+U32 = mybir.dt.uint32
+U16 = mybir.dt.uint16
+U8 = mybir.dt.uint8
+FP8X4 = mybir.dt.float8_e4m3fn_x4
+FP4X4 = mybir.dt.float4_e2m1fn_x4
+MULT = mybir.AluOpType.mult
+ADD = mybir.AluOpType.add
+COPY = mybir.ActivationFunctionType.Copy
+
+P = 128
+D = 512
+T = 2048
+FLOPS = 5 * 2 * D * D * D
+
+
+def tile_picked_decorr_none_po_kernel(
+    tc, x_words, x_scales, wa, wb, gt, gi, w1_words, w1_scales, gk, gq, res, offs, qs, out_0, out_1, out_2
+):
+    nc = tc.nc
+    with ExitStack() as ctx:
+        sb = ctx.enter_context(tc.tile_pool(name="sb", bufs=1))
+        ps = ctx.enter_context(tc.psum_pool(name="ps", bufs=1))
+
+        def sbuf(name, shape, dtype):
+            return sb.tile(shape, dtype, name=name, align_bytes=64)
+
+        def bank(b):
+            return ps.tile([P, D], F32, name="bank%d" % b)
+
+        offs_t = sbuf("offs_t", [P, D // 16], U16)
+        qs_t = sbuf("qs_t", [P, D // 16], U16)
+        xw = sbuf("xw", [P, T], I32)
+        xs = sbuf("xs", [P, T], U8)
+        w1w = sbuf("w1w", [P, 2 * D], U8)
+        w1s = sbuf("w1s", [P, D], U8)
+        wa_raw = [sbuf("wa_raw%d" % h, [P, 4, 256], F32) for h in range(2)]
+        wb_raw = [sbuf("wb_raw%d" % h, [P, 4, 256], F32) for h in range(2)]
+        res_t = sbuf("res_t", [P, 4, D], F32)
+        gate_rows = sbuf("gate_rows", [P, P], F32)
+        ident = sbuf("ident", [P, P], F32)
+
+        nc.gpsimd.memset(xs[:].bitcast(I32), 0)
+        nc.gpsimd.memset(gate_rows[:], 0.0)
+        nc.gpsimd.memset(w1s[:].bitcast(I32), 0)
+        make_identity(nc, ident[:])
+
+        def load_scales(dst, src):
+            for q in range(4):
+                nc.sync.dma_start(dst[32 * q : 32 * q + 4, :].bitcast(I32), src[0, 4 * q : 4 * q + 4, :].bitcast(I32))
+
+        def load_half(dst, w, h):
+            nc.sync.dma_start(dst[h][:], w.rearrange("(p j) c -> p j c", j=4)[:, :, 256 * h : 256 * h + 256])
+
+        def load_gate(g, gate):
+            nc.sync.dma_start(
+                gate_rows[4 * g : 4 * g + 4, :].rearrange("t (q i) -> t q i", i=8),
+                gate.rearrange("(q t i) o -> t q (i o)", t=4, i=8),
+            )
+
+        nc.sync.dma_start(offs_t[:], offs)
+        load_scales(xs, x_scales)
+        nc.sync.dma_start(qs_t[:], qs)
+        nc.sync.dma_start(xw[:], x_words[0].rearrange("p n t -> p (n t)").bitcast(I32))
+        load_half(wa_raw, wa, 0)
+        load_half(wa_raw, wa, 1)
+        for g, gate in enumerate((gt, gi, gq, gk)):
+            load_gate(g, gate)
+        nc.sync.dma_start(w1w[:].bitcast(I32), w1_words[0].bitcast(I32))
+        load_half(wb_raw, wb, 0)
+        load_half(wb_raw, wb, 1)
+        load_scales(w1s, w1_scales)
+        nc.sync.dma_start(res_t[:], res.rearrange("(p t) v -> p t v", t=4))
+
+        def quantise(name, src, width):
+            codes = sbuf(name + "_c", [P, width], U32)
+            scales = sbuf(name + "_s", [P, width], U8)
+            nc.vector.quantize_mx(out=codes[:].bitcast(FP8X4), scales=scales[:], in_=src)
+            return codes, scales
+
+        def mm(out, lw, ls, rw, rs):
+            nc.tensor.matmul_mx(out=out, lhsT=lw, lhsT_scale=ls, rhs=rw, rhs_scale=rs, start=True, stop=True)
+
+        def cols(t):
+            return slice(P * t, P * t + P)
+
+        def project(name, stationary, moving, banks, gate):
+            planes = sbuf(name + "_pl", [P, 4, 256], BF16)
+            for u in range(2):
+                acc = bank(banks[u])
+                for e in range(2):
+                    lw, ls = stationary(2 * u + e)
+                    mm(acc[:, 256 * e : 256 * e + 256], lw, ls, moving[0], moving[1])
+                for e in range(2):
+                    t = 2 * u + e
+                    nc.scalar.activation(planes[:, t, :], acc[:, 256 * e : 256 * e + 256], COPY, scale=gate[:, t : t + 1])
+            return planes
+
+        def direct(dst, stationary, moving, banks, gate):
+            for u in range(2):
+                acc = bank(banks[u])
+                for t in range(4):
+                    lw, ls = stationary(t)
+                    mm(acc[:, cols(t)], lw, ls, moving[0][:, cols(u)].bitcast(FP8X4), moving[1][:, cols(u)])
+                nc.vector.tensor_tensor(
+                    dst[:, 2 * u : 2 * u + 2], acc[:].rearrange("p (t e n) -> p e n t", t=4, e=2),
+                    gate.unsqueeze(1).unsqueeze(1).to_broadcast([P, 2, 64, 4]), MULT,
+                )
+
+        def weave(dst, planes):
+            nc.vector.tensor_copy(
+                dst.rearrange("p e (c i) t -> p e c t i", i=4), planes[:].rearrange("p t (e c i) -> p e c t i", e=4, i=4)
+            )
+
+        def flat(ap):
+            return ap.rearrange("p e n t -> p (e n t)")
+
+        def woven_half(name, planes):
+            woven = sbuf(name + "_wv", [P, 4, 64, 4], BF16)
+            weave(woven[:], planes)
+            return flat(woven[:])
+
+        def whole(q):
+            return q[0][:].bitcast(FP8X4), q[1][:]
+
+        def halves(q):
+            return lambda t: (q[t // 2][0][:, cols(t % 2)].bitcast(FP8X4), q[t // 2][1][:, cols(t % 2)])
+
+        def deal(dst, src):
+            nc.vector.tensor_copy(
+                dst[:].bitcast(I32).rearrange("p (t q w) -> p q t w", t=4, q=16),
+                src[:].bitcast(I32).rearrange("p (q t w) -> p q t w", t=4, q=16),
+            )
+
+        a_s_plain = sbuf("a_s_plain", [P, D], U8)
+        a_s = sbuf("a_s", [P, D], U8)
+        q_s = sbuf("q_s", [P, D], U8)
+        a_w = sbuf("a_w", [P, D], U32)
+        q_w = sbuf("q_w", [P, D], U32)
+        w1w_d = sbuf("w1w_d", [P, 2 * D], U8)
+        w1s_d = sbuf("w1s_d", [P, D], U8)
+        nc.vector.tensor_copy(a_s_plain[:], xs[:].indirect(offs_t[:]))
+        nc.vector.tensor_copy(q_s[:], xs[:].indirect(qs_t[:]))
+        nc.vector.tensor_copy(
+            a_w[:].rearrange("p (t q i) -> p q t i", t=4, i=8), xw[:].bitcast(U32).indirect(offs_t[:])
+        )
+        deal(a_s, a_s_plain)
+        nc.vector.tensor_copy(q_w[:], xw[:].bitcast(U32).indirect(qs_t[:]))
+
+        gate_ps = bank(7)
+        nc.tensor.transpose(gate_ps[:, 0:P], gate_rows[:], ident[:])
+        gates = sbuf("gates", [P, 16], F32)
+        g_t, g_i, g_q, g_k = (gates[:, 4 * g : 4 * g + 4] for g in range(4))
+
+        def x_tile(t):
+            return a_w[:, cols(t)].bitcast(FP8X4), a_s[:, cols(t)]
+
+        def w1_tile(t):
+            return w1w_d[:, 256 * t : 256 * t + 256].bitcast(FP4X4), w1s_d[:, cols(t)]
+
+        def q_cols(lo, n):
+            return q_w[:, lo : lo + n].bitcast(FP8X4), q_s[:, lo : lo + n]
+
+        wa_bf = [sbuf("wa_bf%d" % h, [P, 4, 64, 4], BF16) for h in range(2)]
+        wb_bf = [sbuf("wb_bf%d" % h, [P, 4, 64, 4], BF16) for h in range(2)]
+        z_wv = sbuf("z_wv", [P, 4, P, 4], BF16)
+        z3_wv = sbuf("z3_wv", [P, 4, P, 4], BF16)
+        for h in range(2):
+            nc.scalar.copy(
+                wa_bf[h][:].rearrange("p t (q i) j -> p q t j i", i=8),
+                wa_raw[h][:].rearrange("p j (q t i) -> p q t j i", t=4, i=8),
+            )
+        nc.scalar.copy(gates[:, 0:12], gate_ps[:, 0:12])
+        nc.scalar.activation(g_k, gate_ps[:, 12:16], COPY, scale=0.0625)
+        for h in range(2):
+            nc.scalar.copy(
+                wb_bf[h][:].rearrange("p t m j -> p m j t"), wb_raw[h][:].rearrange("p j (m t) -> p m j t", t=4)
+            )
+        wa_q = [quantise("wa_q%d" % h, flat(wa_bf[h][:]), 256) for h in range(2)]
+        wb_q = [quantise("wb_q%d" % h, flat(wb_bf[h][:]), 256) for h in range(2)]
+        deal(w1w_d, w1w)
+        deal(w1s_d, w1s)
+        for h in range(2):
+            direct(z_wv[:, :, 64 * h : 64 * h + 64], x_tile, wa_q[h], (2 * h, 2 * h + 1), g_t)
+        z2_pl = [project("z2%d" % h, x_tile, whole(wb_q[h]), (4 + 2 * h, 5 + 2 * h), g_i) for h in range(2)]
+        z_q = [quantise("z_q%d" % h, flat(z_wv[:, 2 * h : 2 * h + 2]), 256) for h in range(2)]
+        z2_q = [quantise("z2_q%d" % h, woven_half("z2%d" % h, z2_pl[h]), 256) for h in range(2)]
+        c_pl = [project("c%d" % h, halves(z_q), whole(z2_q[h]), (4 + 2 * h, 5 + 2 * h), g_k) for h in range(2)]
+        for h in range(2):
+            weave(z3_wv[:, :, 64 * h : 64 * h + 64], c_pl[h])
+        z3_q = [quantise("z3_q%d" % h, flat(z3_wv[:, 2 * h : 2 * h + 2]), 256) for h in range(2)]
+        y_pl = project("y0", w1_tile, q_cols(0, 256), (0, 1), g_q)
+        z4_q = [quantise("z4_q0", woven_half("z40", y_pl), 256)]
+        z41 = sbuf("z41_wv", [P, 4, 64, 4], BF16)
+        direct(z41[:], w1_tile, (q_w[:, 256:512], q_s[:, 256:512]), (2, 3), g_q)
+        z4_q.append(quantise("z4_q1", flat(z41[:]), 256))
+
+        out_v = out_0.rearrange("(p t) v -> p t v", t=4)
+        words_v = out_1[0].rearrange("p n t -> p (n t)").bitcast(I32)
+        o_s = sbuf("o_s", [P, D], U8)
+        o_w = sbuf("o_w", [P, D], U32)
+        o_f = [sbuf("o_f%d" % h, [P, 4, 256], F32) for h in range(2)]
+        o_bf = []
+        for c in range(4):
+            acc = bank(4 + c)
+            rw, rs = halves(z4_q)(c)
+            for t in range(4):
+                lw, ls = halves(z3_q)(t)
+                mm(acc[:, cols(t)], lw, ls, rw, rs)
+            o_c = o_f[c // 2][:, :, cols(c % 2)]
+            nc.vector.scalar_tensor_tensor(
+                o_c, acc[:].rearrange("p (t n) -> p t n", t=4), -0.03125, res_t[:, :, cols(c)], MULT, ADD
+            )
+            if c % 2:
+                nc.sync.dma_start(out_v[:, :, 256 * (c // 2) : 256 * (c // 2) + 256], o_f[c // 2][:])
+            woven = sbuf("o_bf%d" % c, [P, P, 4], BF16)
+            cast = nc.vector.tensor_copy if c == 3 else nc.scalar.copy
+            cast(woven[:].rearrange("p (c i) t -> p c t i", i=4), o_c.rearrange("p t (c i) -> p c t i", i=4))
+            o_bf.append(woven)
+        for c in range(4):
+            nc.vector.quantize_mx(
+                out=o_w[:, cols(c)].bitcast(FP8X4), scales=o_s[:, cols(c)], in_=o_bf[c][:].rearrange("p n t -> p (n t)")
+            )
+            if c % 2:
+                nc.sync.dma_start(words_v[:, 256 * (c // 2) : 256 * (c // 2) + 256], o_w[:, 256 * (c // 2) : 256 * (c // 2) + 256].bitcast(I32))
+        for q in range(4):
+            eng = nc.scalar if q % 2 else nc.sync
+            eng.dma_start(out_2[0, 4 * q : 4 * q + 4, :].bitcast(I32), o_s[32 * q : 32 * q + 4, :].bitcast(I32))

@@ -41,15 +41,18 @@ def tile_picked_decorr_none_po_kernel(
         xs = sbuf("xs", [P, T], U8)
         w1w = sbuf("w1w", [P, 2 * D], U8)
         w1s = sbuf("w1s", [P, D], U8)
-        wa_raw = [sbuf("wa_raw%d" % h, [P, 4, 256], F32) for h in range(2)]
+        wa_all = sbuf("wa_all", [P, 4, D], F32)
+        wa_raw = [wa_all[:, :, 256 * h : 256 * h + 256] for h in range(2)]
         wb_raw = [sbuf("wb_raw%d" % h, [P, 4, 256], F32) for h in range(2)]
         res_t = sbuf("res_t", [P, 4, D], F32)
         gate_rows = sbuf("gate_rows", [P, P], F32)
+        g_t = sbuf("g_t", [P, 4], F32)
+        g_i = sbuf("g_i", [P, 4], F32)
         ident = sbuf("ident", [P, P], F32)
 
         nc.gpsimd.memset(xs[:].bitcast(I32), 0)
-        nc.gpsimd.memset(gate_rows[:], 0.0)
-        nc.gpsimd.memset(w1s[:].bitcast(I32), 0)
+        nc.vector.memset(gate_rows[:], 0.0)
+        nc.vector.memset(w1s[:].bitcast(I32), 0)
         make_identity(nc, ident[:])
 
         def load_scales(dst, src):
@@ -69,13 +72,14 @@ def tile_picked_decorr_none_po_kernel(
         load_scales(xs, x_scales)
         nc.sync.dma_start(qs_t[:], qs)
         nc.sync.dma_start(xw[:], x_words[0].rearrange("p n t -> p (n t)").bitcast(I32))
-        load_half(wa_raw, wa, 0)
-        load_half(wa_raw, wa, 1)
-        for g, gate in enumerate((gt, gi, gq, gk)):
-            load_gate(g, gate)
-        nc.sync.dma_start(w1w[:].bitcast(I32), w1_words[0].bitcast(I32))
+        nc.sync.dma_start(wa_all[:], wa.rearrange("(p j) c -> p j c", j=4))
+        nc.sync.dma_start(g_t[:], gt.rearrange("(p t) o -> p (t o)", t=4))
+        nc.sync.dma_start(g_i[:], gi.rearrange("(p t) o -> p (t o)", t=4))
         load_half(wb_raw, wb, 0)
         load_half(wb_raw, wb, 1)
+        for g, gate in enumerate((gq, gk)):
+            load_gate(g, gate)
+        nc.sync.dma_start(w1w[:].bitcast(I32), w1_words[0].bitcast(I32))
         load_scales(w1s, w1_scales)
         nc.sync.dma_start(res_t[:], res.rearrange("(p t) v -> p t v", t=4))
 
@@ -111,7 +115,7 @@ def tile_picked_decorr_none_po_kernel(
                     mm(acc[:, cols(t)], lw, ls, moving[0][:, cols(u)].bitcast(FP8X4), moving[1][:, cols(u)])
                 nc.vector.tensor_tensor(
                     dst[:, 2 * u : 2 * u + 2], acc[:].rearrange("p (t e n) -> p e n t", t=4, e=2),
-                    gate.unsqueeze(1).unsqueeze(1).to_broadcast([P, 2, 64, 4]), MULT,
+                    gate[:].unsqueeze(1).unsqueeze(1).to_broadcast([P, 2, 64, 4]), MULT,
                 )
 
         def weave(dst, planes):
@@ -149,15 +153,11 @@ def tile_picked_decorr_none_po_kernel(
         nc.vector.tensor_copy(a_s_plain[:], xs[:].indirect(offs_t[:]))
         nc.vector.tensor_copy(q_s[:], xs[:].indirect(qs_t[:]))
         nc.vector.tensor_copy(
-            a_w[:].rearrange("p (t q i) -> p q t i", t=4, i=8), xw[:].bitcast(U32).indirect(offs_t[:])
+            a_w[:].rearrange("p (t m) -> p m t", t=4), xw[:].bitcast(U32).indirect(offs_t[:])
         )
-        deal(a_s, a_s_plain)
+        nc.vector.tensor_copy(a_s[:].rearrange("p (t m) -> p m t", t=4), a_s_plain[:].rearrange("p (m t) -> p m t", t=4))
         nc.vector.tensor_copy(q_w[:], xw[:].bitcast(U32).indirect(qs_t[:]))
 
-        gate_ps = bank(7)
-        nc.tensor.transpose(gate_ps[:, 0:P], gate_rows[:], ident[:])
-        gates = sbuf("gates", [P, 16], F32)
-        g_t, g_i, g_q, g_k = (gates[:, 4 * g : 4 * g + 4] for g in range(4))
 
         def x_tile(t):
             return a_w[:, cols(t)].bitcast(FP8X4), a_s[:, cols(t)]
@@ -173,63 +173,73 @@ def tile_picked_decorr_none_po_kernel(
         z_wv = sbuf("z_wv", [P, 4, P, 4], BF16)
         z3_wv = sbuf("z3_wv", [P, 4, P, 4], BF16)
         for h in range(2):
-            nc.scalar.copy(
+            cast = nc.vector.tensor_copy if h else nc.scalar.copy
+            cast(
                 wa_bf[h][:].rearrange("p t (q i) j -> p q t j i", i=8),
-                wa_raw[h][:].rearrange("p j (q t i) -> p q t j i", t=4, i=8),
+                wa_raw[h].rearrange("p j (q t i) -> p q t j i", t=4, i=8),
             )
-        nc.scalar.copy(gates[:, 0:12], gate_ps[:, 0:12])
-        nc.scalar.activation(g_k, gate_ps[:, 12:16], COPY, scale=0.0625)
+        wb_q = []
         for h in range(2):
-            nc.scalar.copy(
-                wb_bf[h][:].rearrange("p t m j -> p m j t"), wb_raw[h][:].rearrange("p j (m t) -> p m j t", t=4)
-            )
+            cast = nc.vector.tensor_copy if h else nc.scalar.copy
+            cast(wb_bf[h][:].rearrange("p t m j -> p m j t"), wb_raw[h][:].rearrange("p j (m t) -> p m j t", t=4))
+            wb_q.append(quantise("wb_q%d" % h, flat(wb_bf[h][:]), 256))
         wa_q = [quantise("wa_q%d" % h, flat(wa_bf[h][:]), 256) for h in range(2)]
-        wb_q = [quantise("wb_q%d" % h, flat(wb_bf[h][:]), 256) for h in range(2)]
-        deal(w1w_d, w1w)
-        deal(w1s_d, w1s)
-        for h in range(2):
-            direct(z_wv[:, :, 64 * h : 64 * h + 64], x_tile, wa_q[h], (2 * h, 2 * h + 1), g_t)
         z2_pl = [project("z2%d" % h, x_tile, whole(wb_q[h]), (4 + 2 * h, 5 + 2 * h), g_i) for h in range(2)]
+        direct(z_wv[:, :, 64:128], x_tile, wa_q[1], (0, 1), g_t)
+        weave(z_wv[:, :, 0:64], project("z0", x_tile, whole(wa_q[0]), (2, 3), g_t))
+        gate_ps = bank(0)
+        nc.tensor.transpose(gate_ps[:, 0:P], gate_rows[:], ident[:])
+        g_q = sbuf("g_q", [P, 4], F32)
+        g_k = sbuf("g_k", [P, 4], F32)
+        nc.scalar.copy(g_q[:], gate_ps[:, 0:4])
+        nc.scalar.activation(g_k[:], gate_ps[:, 4:8], COPY, scale=0.0625)
+        z2_wv0 = woven_half("z20", z2_pl[0])
         z_q = [quantise("z_q%d" % h, flat(z_wv[:, 2 * h : 2 * h + 2]), 256) for h in range(2)]
-        z2_q = [quantise("z2_q%d" % h, woven_half("z2%d" % h, z2_pl[h]), 256) for h in range(2)]
-        c_pl = [project("c%d" % h, halves(z_q), whole(z2_q[h]), (4 + 2 * h, 5 + 2 * h), g_k) for h in range(2)]
+        z2_q = [quantise("z2_q0", z2_wv0, 256), quantise("z2_q1", woven_half("z21", z2_pl[1]), 256)]
+        c_pl = [project("c%d" % h, halves(z_q), whole(z2_q[h]), (2 + 2 * h, 3 + 2 * h), g_k) for h in range(2)]
         for h in range(2):
             weave(z3_wv[:, :, 64 * h : 64 * h + 64], c_pl[h])
         z3_q = [quantise("z3_q%d" % h, flat(z3_wv[:, 2 * h : 2 * h + 2]), 256) for h in range(2)]
-        y_pl = project("y0", w1_tile, q_cols(0, 256), (0, 1), g_q)
-        z4_q = [quantise("z4_q0", woven_half("z40", y_pl), 256)]
-        z41 = sbuf("z41_wv", [P, 4, 64, 4], BF16)
-        direct(z41[:], w1_tile, (q_w[:, 256:512], q_s[:, 256:512]), (2, 3), g_q)
-        z4_q.append(quantise("z4_q1", flat(z41[:]), 256))
+        deal(w1w_d, w1w)
+        deal(w1s_d, w1s)
+        z40 = sbuf("z21_wv", [P, 4, 64, 4], BF16)
+        direct(z40[:], w1_tile, (q_w[:, 0:256], q_s[:, 0:256]), (6, 7), g_q)
+        z4_q = [quantise("z4_q0", flat(z40[:]), 256)]
+        y_pl = project("y1", w1_tile, q_cols(256, 256), (0, 1), g_q)
+        z4_q.append(quantise("z4_q1", woven_half("z41", y_pl), 256))
 
         out_v = out_0.rearrange("(p t) v -> p t v", t=4)
         words_v = out_1[0].rearrange("p n t -> p (n t)").bitcast(I32)
         o_s = sbuf("o_s", [P, D], U8)
         o_w = sbuf("o_w", [P, D], U32)
         o_f = [sbuf("o_f%d" % h, [P, 4, 256], F32) for h in range(2)]
-        o_bf = []
-        for c in range(4):
-            acc = bank(4 + c)
-            rw, rs = halves(z4_q)(c)
-            for t in range(4):
-                lw, ls = halves(z3_q)(t)
-                mm(acc[:, cols(t)], lw, ls, rw, rs)
-            o_c = o_f[c // 2][:, :, cols(c % 2)]
-            nc.vector.scalar_tensor_tensor(
-                o_c, acc[:].rearrange("p (t n) -> p t n", t=4), -0.03125, res_t[:, :, cols(c)], MULT, ADD
-            )
-            if c % 2:
-                nc.sync.dma_start(out_v[:, :, 256 * (c // 2) : 256 * (c // 2) + 256], o_f[c // 2][:])
-            woven = sbuf("o_bf%d" % c, [P, P, 4], BF16)
-            cast = nc.vector.tensor_copy if c == 3 else nc.scalar.copy
-            cast(woven[:].rearrange("p (c i) t -> p c t i", i=4), o_c.rearrange("p t (c i) -> p c t i", i=4))
-            o_bf.append(woven)
-        for c in range(4):
+        o_bf = [sbuf("o_bf%d" % c, [P, P, 4], BF16) for c in range(4)]
+        for h in range(2):
+            v_half = slice(256 * h, 256 * h + 256)
+            for u in range(2):
+                acc = bank(2 + 2 * h + u)
+                rw, rs = whole(z4_q[h])
+                for e in range(2):
+                    lw, ls = halves(z3_q)(2 * u + e)
+                    mm(acc[:, 256 * e : 256 * e + 256], lw, ls, rw, rs)
+                nc.vector.scalar_tensor_tensor(
+                    o_f[h][:, 2 * u : 2 * u + 2], acc[:].rearrange("p (e n) -> p e n", e=2), -0.03125,
+                    res_t[:, 2 * u : 2 * u + 2, v_half], MULT, ADD,
+                )
+                nc.sync.dma_start(out_v[:, 2 * u : 2 * u + 2, v_half], o_f[h][:, 2 * u : 2 * u + 2])
+            for c in (2 * h, 2 * h + 1):
+                cast = nc.vector.tensor_copy if c == 3 else nc.scalar.copy
+                cast(
+                    o_bf[c][:].rearrange("p (c i) t -> p c t i", i=4),
+                    o_f[h][:, :, cols(c % 2)].rearrange("p t (c i) -> p c t i", i=4),
+                )
+        for c in (0, 1, 3, 2):
             nc.vector.quantize_mx(
                 out=o_w[:, cols(c)].bitcast(FP8X4), scales=o_s[:, cols(c)], in_=o_bf[c][:].rearrange("p n t -> p (n t)")
             )
-            if c % 2:
-                nc.sync.dma_start(words_v[:, 256 * (c // 2) : 256 * (c // 2) + 256], o_w[:, 256 * (c // 2) : 256 * (c // 2) + 256].bitcast(I32))
+            if c in (1, 2):
+                v_half = slice(256 * (c // 2), 256 * (c // 2) + 256)
+                nc.sync.dma_start(words_v[:, v_half], o_w[:, v_half].bitcast(I32))
         for q in range(4):
             eng = nc.scalar if q % 2 else nc.sync
             eng.dma_start(out_2[0, 4 * q : 4 * q + 4, :].bitcast(I32), o_s[32 * q : 32 * q + 4, :].bitcast(I32))

@@ -29,8 +29,8 @@ def tile_picked_decorr_none_po_kernel(
         sb = ctx.enter_context(tc.tile_pool(name="sb", bufs=1))
         ps = ctx.enter_context(tc.psum_pool(name="ps", bufs=1))
 
-        def sbuf(name, shape, dtype):
-            return sb.tile(shape, dtype, name=name, align_bytes=64)
+        def sbuf(name, shape, dtype, slot=None):
+            return sb.tile(shape, dtype, name=name, tag=slot or name, align_bytes=64)
 
         def bank(b):
             return ps.tile([P, D], F32, name="bank%d" % b)
@@ -114,13 +114,19 @@ def tile_picked_decorr_none_po_kernel(
                     lw, ls = stationary(t)
                     mm(acc[:, cols(t)], lw, ls, moving[0][:, cols(u)].bitcast(FP8X4), moving[1][:, cols(u)])
                 nc.vector.tensor_tensor(
-                    dst[:, 2 * u : 2 * u + 2], acc[:].rearrange("p (t e n) -> p e n t", t=4, e=2),
+                    dst(u), acc[:].rearrange("p (t e n) -> p e n t", t=4, e=2),
                     gate[:].unsqueeze(1).unsqueeze(1).to_broadcast([P, 2, 64, 4]), MULT,
                 )
 
         def weave(dst, planes):
             nc.vector.tensor_copy(
                 dst.rearrange("p e (c i) t -> p e c t i", i=4), planes[:].rearrange("p t (e c i) -> p e c t i", e=4, i=4)
+            )
+
+        def weave_pair(dst, planes, u):
+            nc.vector.tensor_copy(
+                dst.rearrange("p e (c i) t -> p e c t i", i=4),
+                planes[:, :, cols(u)].rearrange("p t (e c i) -> p e c t i", e=2, i=4),
             )
 
         def flat(ap):
@@ -147,17 +153,19 @@ def tile_picked_decorr_none_po_kernel(
         a_s = sbuf("a_s", [P, D], U8)
         q_s = sbuf("q_s", [P, D], U8)
         a_w = sbuf("a_w", [P, D], U32)
-        q_w = sbuf("q_w", [P, D], U32)
-        w1w_d = sbuf("w1w_d", [P, 2 * D], U8)
-        w1s_d = sbuf("w1s_d", [P, D], U8)
         nc.vector.tensor_copy(a_s_plain[:], xs[:].indirect(offs_t[:]))
         nc.vector.tensor_copy(q_s[:], xs[:].indirect(qs_t[:]))
         nc.vector.tensor_copy(
             a_w[:].rearrange("p (t m) -> p m t", t=4), xw[:].bitcast(U32).indirect(offs_t[:])
         )
         nc.vector.tensor_copy(a_s[:].rearrange("p (t m) -> p m t", t=4), a_s_plain[:].rearrange("p (m t) -> p m t", t=4))
-        nc.vector.tensor_copy(q_w[:], xw[:].bitcast(U32).indirect(qs_t[:]))
+        q_w = [sbuf("q_w0", [P, 256], U32)]
+        nc.vector.tensor_copy(q_w[0][:], xw[:].bitcast(U32).indirect(qs_t[:, 0:16]))
 
+
+        warm = bank(7)
+        for r in range(3):
+            mm(warm[:], a_w[:, cols(r)].bitcast(FP8X4), a_s[:, cols(r)], a_w[:].bitcast(FP8X4), a_s[:])
 
         def x_tile(t):
             return a_w[:, cols(t)].bitcast(FP8X4), a_s[:, cols(t)]
@@ -166,11 +174,9 @@ def tile_picked_decorr_none_po_kernel(
             return w1w_d[:, 256 * t : 256 * t + 256].bitcast(FP4X4), w1s_d[:, cols(t)]
 
         def q_cols(lo, n):
-            return q_w[:, lo : lo + n].bitcast(FP8X4), q_s[:, lo : lo + n]
+            return q_w[lo // n][:].bitcast(FP8X4), q_s[:, lo : lo + n]
 
         wa_bf = [sbuf("wa_bf%d" % h, [P, 4, 64, 4], BF16) for h in range(2)]
-        wb_bf = [sbuf("wb_bf%d" % h, [P, 4, 64, 4], BF16) for h in range(2)]
-        z_wv = sbuf("z_wv", [P, 4, P, 4], BF16)
         z3_wv = sbuf("z3_wv", [P, 4, P, 4], BF16)
         for h in range(2):
             cast = nc.vector.tensor_copy if h else nc.scalar.copy
@@ -178,34 +184,45 @@ def tile_picked_decorr_none_po_kernel(
                 wa_bf[h][:].rearrange("p t (q i) j -> p q t j i", i=8),
                 wa_raw[h].rearrange("p j (q t i) -> p q t j i", t=4, i=8),
             )
+        wa_q = [quantise("wa_q%d" % h, flat(wa_bf[h][:]), 256) for h in range(2)]
+        q_w.append(sbuf("q_w1", [P, 256], U32, slot="wa_bf1"))
+        nc.vector.tensor_copy(q_w[1][:], xw[:].bitcast(U32).indirect(qs_t[:, 16:32]))
         wb_q = []
         for h in range(2):
+            wb_bf = sbuf("wb_bf%d" % h, [P, 4, 64, 4], BF16, slot="wb_bf")
             cast = nc.vector.tensor_copy if h else nc.scalar.copy
-            cast(wb_bf[h][:].rearrange("p t m j -> p m j t"), wb_raw[h][:].rearrange("p j (m t) -> p m j t", t=4))
-            wb_q.append(quantise("wb_q%d" % h, flat(wb_bf[h][:]), 256))
-        wa_q = [quantise("wa_q%d" % h, flat(wa_bf[h][:]), 256) for h in range(2)]
+            cast(wb_bf[:].rearrange("p t m j -> p m j t"), wb_raw[h][:].rearrange("p j (m t) -> p m j t", t=4))
+            wb_q.append(quantise("wb_q%d" % h, flat(wb_bf[:]), 256))
+        w1w_d = sbuf("w1w_d", [P, 2 * D], U8, slot="wb_bf")
+        z_wv = [sbuf("z_wv0", [P, 2, P, 4], BF16), sbuf("z_wv1", [P, 2, P, 4], BF16, slot="wb_raw1")]
+        direct(lambda u: z_wv[u][:, :, 64:128], x_tile, wa_q[1], (0, 1), g_t)
+        deal(w1w_d, w1w)
+        z_pl = project("z0", x_tile, whole(wa_q[0]), (2, 3), g_t)
         z2_pl = [project("z2%d" % h, x_tile, whole(wb_q[h]), (4 + 2 * h, 5 + 2 * h), g_i) for h in range(2)]
-        direct(z_wv[:, :, 64:128], x_tile, wa_q[1], (0, 1), g_t)
-        weave(z_wv[:, :, 0:64], project("z0", x_tile, whole(wa_q[0]), (2, 3), g_t))
         gate_ps = bank(0)
         nc.tensor.transpose(gate_ps[:, 0:P], gate_rows[:], ident[:])
         g_q = sbuf("g_q", [P, 4], F32)
         g_k = sbuf("g_k", [P, 4], F32)
         nc.scalar.copy(g_q[:], gate_ps[:, 0:4])
         nc.scalar.activation(g_k[:], gate_ps[:, 4:8], COPY, scale=0.0625)
+        for u in range(2):
+            weave_pair(z_wv[u][:, :, 0:64], z_pl, u)
+        w1s_d = sbuf("w1s_d", [P, D], U8, slot="z0_pl")
+        deal(w1s_d, w1s)
+        y_pl = project("y0", w1_tile, q_cols(0, 256), (0, 1), g_q)
         z2_wv0 = woven_half("z20", z2_pl[0])
-        z_q = [quantise("z_q%d" % h, flat(z_wv[:, 2 * h : 2 * h + 2]), 256) for h in range(2)]
+        z_q = [quantise("z_q%d" % h, flat(z_wv[h][:]), 256) for h in range(2)]
         z2_q = [quantise("z2_q0", z2_wv0, 256), quantise("z2_q1", woven_half("z21", z2_pl[1]), 256)]
         c_pl = [project("c%d" % h, halves(z_q), whole(z2_q[h]), (2 + 2 * h, 3 + 2 * h), g_k) for h in range(2)]
-        for h in range(2):
-            weave(z3_wv[:, :, 64 * h : 64 * h + 64], c_pl[h])
+        weave(z3_wv[:, :, 0:64], c_pl[0])
+        for u in range(2):
+            nc.vector.tensor_copy(
+                z3_wv[:, 2 * u : 2 * u + 2, 64:128].rearrange("p e (c i) t -> p e c t i", i=4),
+                c_pl[1][:, :, cols(u)].rearrange("p t (e c i) -> p e c t i", e=2, i=4),
+            )
         z3_q = [quantise("z3_q%d" % h, flat(z3_wv[:, 2 * h : 2 * h + 2]), 256) for h in range(2)]
-        deal(w1w_d, w1w)
-        deal(w1s_d, w1s)
-        z40 = sbuf("z21_wv", [P, 4, 64, 4], BF16)
-        direct(z40[:], w1_tile, (q_w[:, 0:256], q_s[:, 0:256]), (6, 7), g_q)
-        z4_q = [quantise("z4_q0", flat(z40[:]), 256)]
-        y_pl = project("y1", w1_tile, q_cols(256, 256), (0, 1), g_q)
+        z4_q = [quantise("z4_q0", woven_half("z40", y_pl), 256)]
+        y_pl = project("y1", w1_tile, q_cols(256, 256), (6, 7), g_q)
         z4_q.append(quantise("z4_q1", woven_half("z41", y_pl), 256))
 
         out_v = out_0.rearrange("(p t) v -> p t v", t=4)

@@ -17,6 +17,7 @@ COPY = mybir.ActivationFunctionType.Copy
 
 P = 128
 D = 512
+H = 256
 T = 2048
 FLOPS = 5 * 2 * D * D * D
 
@@ -35,228 +36,224 @@ def tile_picked_decorr_none_po_kernel(
         def bank(b):
             return ps.tile([P, D], F32, name="bank%d" % b)
 
+        def cols(t, n=P):
+            return slice(n * t, n * t + n)
+
         offs_t = sbuf("offs_t", [P, D // 16], U16)
         qs_t = sbuf("qs_t", [P, D // 16], U16)
         xw = sbuf("xw", [P, T], I32)
         xs = sbuf("xs", [P, T], U8)
+        wa_raw = sbuf("wa_raw", [P, 4, D], F32)
         w1w = sbuf("w1w", [P, 2 * D], U8)
-        w1s = sbuf("w1s", [P, D], U8)
-        wa_all = sbuf("wa_all", [P, 4, D], F32)
-        wa_raw = [wa_all[:, :, 256 * h : 256 * h + 256] for h in range(2)]
-        wb_raw = [sbuf("wb_raw%d" % h, [P, 4, 256], F32) for h in range(2)]
-        res_t = sbuf("res_t", [P, 4, D], F32)
-        gate_rows = sbuf("gate_rows", [P, P], F32)
-        g_t = sbuf("g_t", [P, 4], F32)
-        g_i = sbuf("g_i", [P, 4], F32)
+        gate_rows = sbuf("gate_rows", [P, D], F32)
         ident = sbuf("ident", [P, P], F32)
+        picked_s = sbuf("picked_s", [P, 2 * D], U8)
+        plane_s = sbuf("plane_s", [P, 2 * D], U8)
 
-        nc.gpsimd.memset(xs[:].bitcast(I32), 0)
-        nc.vector.memset(gate_rows[:], 0.0)
-        nc.vector.memset(w1s[:].bitcast(I32), 0)
+        nc.gpsimd.memset(xs[0 : P - 16, :].bitcast(I32), 0)
+        nc.vector.memset(gate_rows[0 : P - 4, :], 0.0)
+        nc.vector.memset(plane_s[:].bitcast(I32), 0)
         make_identity(nc, ident[:])
 
-        def load_scales(dst, src):
-            for q in range(4):
+        def load_scales(dst, src, quads):
+            for q in quads:
                 nc.sync.dma_start(dst[32 * q : 32 * q + 4, :].bitcast(I32), src[0, 4 * q : 4 * q + 4, :].bitcast(I32))
 
-        def load_half(dst, w, h):
-            nc.sync.dma_start(dst[h][:], w.rearrange("(p j) c -> p j c", j=4)[:, :, 256 * h : 256 * h + 256])
+        def load_rows(dst, w):
+            nc.sync.dma_start(dst[:], w.rearrange("(p j) c -> p j c", j=4))
 
-        def load_gate(g, gate):
-            nc.sync.dma_start(
-                gate_rows[4 * g : 4 * g + 4, :].rearrange("t (q i) -> t q i", i=8),
-                gate.rearrange("(q t i) o -> t q (i o)", t=4, i=8),
-            )
-
+        nc.sync.dma_start(xs[P - 16 : P, :].bitcast(I32), x_scales[0].bitcast(I32))
         nc.sync.dma_start(offs_t[:], offs)
-        load_scales(xs, x_scales)
         nc.sync.dma_start(qs_t[:], qs)
         nc.sync.dma_start(xw[:], x_words[0].rearrange("p n t -> p (n t)").bitcast(I32))
-        nc.sync.dma_start(wa_all[:], wa.rearrange("(p j) c -> p j c", j=4))
-        nc.sync.dma_start(g_t[:], gt.rearrange("(p t) o -> p (t o)", t=4))
-        nc.sync.dma_start(g_i[:], gi.rearrange("(p t) o -> p (t o)", t=4))
-        load_half(wb_raw, wb, 0)
-        load_half(wb_raw, wb, 1)
-        for g, gate in enumerate((gq, gk)):
-            load_gate(g, gate)
+        for g, gate in enumerate((gt, gi, gq, gk)):
+            nc.sync.dma_start(gate_rows[P - 4 + g : P - 3 + g, :], gate.rearrange("n o -> o n"))
+        load_rows(wa_raw, wa)
         nc.sync.dma_start(w1w[:].bitcast(I32), w1_words[0].bitcast(I32))
-        load_scales(w1s, w1_scales)
-        nc.sync.dma_start(res_t[:], res.rearrange("(p t) v -> p t v", t=4))
 
-        def quantise(name, src, width):
-            codes = sbuf(name + "_c", [P, width], U32)
-            scales = sbuf(name + "_s", [P, width], U8)
-            nc.vector.quantize_mx(out=codes[:].bitcast(FP8X4), scales=scales[:], in_=src)
+        gate_dealt = sbuf("gate_dealt", [P, 4, P], F32)
+        nc.scalar.copy(
+            gate_dealt[:].rearrange("g t (u r) -> g t u r", r=4), gate_rows[:].rearrange("g (u t r) -> g t u r", t=4, r=4)
+        )
+        gate_ps = bank(7)
+        for t in range(4):
+            nc.tensor.transpose(gate_ps[:, cols(t)], gate_dealt[:, t], ident[:])
+        gates = sbuf("gates", [P, 3, 4], F32)
+        g_k = sbuf("g_k", [P, 4], F32)
+        turned = gate_ps[:].rearrange("p (t g) -> p g t", t=4)
+        nc.scalar.copy(gates[:], turned[:, P - 4 : P - 1])
+        nc.scalar.activation(g_k[:], turned[:, P - 1], COPY, scale=0.0625)
+        g_t, g_i, g_q = gates[:, 0], gates[:, 1], gates[:, 2]
+
+        def flat(ap):
+            return ap.rearrange("p n t -> p (n t)")
+
+        def quantise(name, woven, slot=None):
+            codes = sbuf(name + "_c", [P, H], U32, slot)
+            scales = sbuf(name + "_s", [P, H], U8)
+            nc.vector.quantize_mx(out=codes[:].bitcast(FP8X4), scales=scales[:], in_=flat(woven[:]))
             return codes, scales
 
         def mm(out, lw, ls, rw, rs):
             nc.tensor.matmul_mx(out=out, lhsT=lw, lhsT_scale=ls, rhs=rw, rhs_scale=rs, start=True, stop=True)
 
-        def cols(t):
-            return slice(P * t, P * t + P)
-
-        def project(name, stationary, moving, banks, gate):
-            planes = sbuf(name + "_pl", [P, 4, 256], BF16)
+        def planes(name, stationary, moving, banks, gate):
+            pl = sbuf(name + "_pl", [P, 4, H], BF16)
             for u in range(2):
                 acc = bank(banks[u])
                 for e in range(2):
                     lw, ls = stationary(2 * u + e)
-                    mm(acc[:, 256 * e : 256 * e + 256], lw, ls, moving[0], moving[1])
+                    mm(acc[:, cols(e, H)], lw, ls, moving[0].bitcast(FP8X4), moving[1])
                 for e in range(2):
                     t = 2 * u + e
-                    nc.scalar.activation(planes[:, t, :], acc[:, 256 * e : 256 * e + 256], COPY, scale=gate[:, t : t + 1])
-            return planes
+                    nc.scalar.activation(pl[:, t, :], acc[:, cols(e, H)], COPY, scale=gate[:, t : t + 1])
+            return pl
 
-        def direct(dst, stationary, moving, banks, gate):
-            for u in range(2):
-                acc = bank(banks[u])
-                for t in range(4):
-                    lw, ls = stationary(t)
-                    mm(acc[:, cols(t)], lw, ls, moving[0][:, cols(u)].bitcast(FP8X4), moving[1][:, cols(u)])
-                nc.vector.tensor_tensor(
-                    dst(u), acc[:].rearrange("p (t e n) -> p e n t", t=4, e=2),
-                    gate[:].unsqueeze(1).unsqueeze(1).to_broadcast([P, 2, 64, 4]), MULT,
-                )
-
-        def weave(dst, planes):
+        def weave(name, pl, slot=None):
+            woven = sbuf(name + "_wv", [P, H, 4], BF16, slot)
             nc.vector.tensor_copy(
-                dst.rearrange("p e (c i) t -> p e c t i", i=4), planes[:].rearrange("p t (e c i) -> p e c t i", e=4, i=4)
+                woven[:].rearrange("p (c i) t -> p c t i", i=4), pl[:].rearrange("p t (c i) -> p c t i", i=4)
             )
+            return woven
 
-        def weave_pair(dst, planes, u):
-            nc.vector.tensor_copy(
-                dst.rearrange("p e (c i) t -> p e c t i", i=4),
-                planes[:, :, cols(u)].rearrange("p t (e c i) -> p e c t i", e=2, i=4),
+        def direct_bank(dst, u, stationary, moving, b, gate):
+            acc = bank(b)
+            for t in range(4):
+                lw, ls = stationary(t)
+                mm(acc[:, cols(t)], lw, ls, moving[0][:, cols(u)].bitcast(FP8X4), moving[1][:, cols(u)])
+            nc.vector.tensor_tensor(
+                dst, acc[:].rearrange("p (t n) -> p n t", t=4),
+                gate.unsqueeze(1).to_broadcast([P, P, 4]), MULT,
             )
-
-        def flat(ap):
-            return ap.rearrange("p e n t -> p (e n t)")
-
-        def woven_half(name, planes):
-            woven = sbuf(name + "_wv", [P, 4, 64, 4], BF16)
-            weave(woven[:], planes)
-            return flat(woven[:])
 
         def whole(q):
-            return q[0][:].bitcast(FP8X4), q[1][:]
+            return q[0][:], q[1][:]
 
-        def halves(q):
+        def tiles_of(q):
             return lambda t: (q[t // 2][0][:, cols(t % 2)].bitcast(FP8X4), q[t // 2][1][:, cols(t % 2)])
 
         def deal(dst, src):
             nc.vector.tensor_copy(
-                dst[:].bitcast(I32).rearrange("p (t q w) -> p q t w", t=4, q=16),
-                src[:].bitcast(I32).rearrange("p (q t w) -> p q t w", t=4, q=16),
+                dst.bitcast(I32).rearrange("p (t u w) -> p t u w", t=4, u=32),
+                src.bitcast(I32).rearrange("p (u t w) -> p t u w", t=4, u=32),
             )
 
-        a_s_plain = sbuf("a_s_plain", [P, D], U8)
         a_s = sbuf("a_s", [P, D], U8)
-        q_s = sbuf("q_s", [P, D], U8)
         a_w = sbuf("a_w", [P, D], U32)
-        nc.vector.tensor_copy(a_s_plain[:], xs[:].indirect(offs_t[:]))
-        nc.vector.tensor_copy(q_s[:], xs[:].indirect(qs_t[:]))
+        q_w = sbuf("q_w", [P, D], U32)
+        w1w_d = sbuf("w1w_d", [P, 2 * D], U8)
+        w1s_d = sbuf("w1s_d", [P, D], U8)
+        nc.vector.tensor_copy(picked_s[:, 0:D], xs[:].indirect(offs_t[:]))
+        nc.vector.tensor_copy(picked_s[:, D : 2 * D], xs[:].indirect(qs_t[:]))
+        for q in range(4):
+            nc.sync.dma_start(
+                plane_s[32 * q : 32 * q + 4, :].bitcast(I32), picked_s[P - 16 + 4 * q : P - 12 + 4 * q, :].bitcast(I32)
+            )
+        wb_raw = sbuf("wb_raw", [P, 4, D], F32, "xs")
+        load_rows(wb_raw, wb)
         nc.vector.tensor_copy(
-            a_w[:].rearrange("p (t m) -> p m t", t=4), xw[:].bitcast(U32).indirect(offs_t[:])
+            a_w[:].rearrange("p (t u r) -> p u t r", t=4, r=4), xw[:].bitcast(U32).indirect(offs_t[:])
         )
-        nc.vector.tensor_copy(a_s[:].rearrange("p (t m) -> p m t", t=4), a_s_plain[:].rearrange("p (m t) -> p m t", t=4))
-        q_w = [sbuf("q_w0", [P, 256], U32)]
-        nc.vector.tensor_copy(q_w[0][:], xw[:].bitcast(U32).indirect(qs_t[:, 0:16]))
-
-
-        warm = bank(7)
-        for r in range(3):
-            mm(warm[:], a_w[:, cols(r)].bitcast(FP8X4), a_s[:, cols(r)], a_w[:].bitcast(FP8X4), a_s[:])
+        nc.vector.tensor_copy(q_w[:], xw[:].bitcast(U32).indirect(qs_t[:]))
+        deal(a_s[:], plane_s[:, 0:D])
+        w1s = sbuf("w1s", [P, D], U8, "xw")
+        nc.gpsimd.memset(w1s[:].bitcast(I32), 0)
+        load_scales(w1s, w1_scales, range(4))
 
         def x_tile(t):
             return a_w[:, cols(t)].bitcast(FP8X4), a_s[:, cols(t)]
 
         def w1_tile(t):
-            return w1w_d[:, 256 * t : 256 * t + 256].bitcast(FP4X4), w1s_d[:, cols(t)]
+            return w1w_d[:, cols(t, H)].bitcast(FP4X4), w1s_d[:, cols(t)]
 
-        def q_cols(lo, n):
-            return q_w[lo // n][:].bitcast(FP8X4), q_s[:, lo : lo + n]
+        def q_half(h):
+            return q_w[:, cols(h, H)], plane_s[:, cols(2 + h, H)]
 
-        wa_bf = [sbuf("wa_bf%d" % h, [P, 4, 64, 4], BF16) for h in range(2)]
-        z3_wv = sbuf("z3_wv", [P, 4, P, 4], BF16)
-        for h in range(2):
-            cast = nc.vector.tensor_copy if h else nc.scalar.copy
+        def round_wa(h, cast, slot=None):
+            dst = sbuf("wa_bf%d" % h, [P, H, 4], BF16, slot)
             cast(
-                wa_bf[h][:].rearrange("p t (q i) j -> p q t j i", i=8),
-                wa_raw[h].rearrange("p j (q t i) -> p q t j i", t=4, i=8),
+                dst[:].rearrange("p (t u r) j -> p t u j r", t=2, r=4),
+                wa_raw[:].rearrange("p j (u t r) -> p t u j r", t=4, r=4)[:, 2 * h : 2 * h + 2],
             )
-        wa_q = [quantise("wa_q%d" % h, flat(wa_bf[h][:]), 256) for h in range(2)]
-        q_w.append(sbuf("q_w1", [P, 256], U32, slot="wa_bf1"))
-        nc.vector.tensor_copy(q_w[1][:], xw[:].bitcast(U32).indirect(qs_t[:, 16:32]))
-        wb_q = []
+            return dst
+
+        def round_wb(h, cast):
+            dst = z_wv[:, cols(2 * h, H)]
+            cast(
+                dst.rearrange("p (t m) j -> p m j t", t=2),
+                wb_raw[:].rearrange("p j (m t) -> p m j t", t=4)[:, :, :, 2 * h : 2 * h + 2],
+            )
+            return dst
+
+        warm = bank(6)
+        for r in range(3):
+            mm(warm[:], q_w[:, cols(r)].bitcast(FP8X4), plane_s[:, cols(4 + r)], q_w[:].bitcast(FP8X4), plane_s[:, cols(1, D)])
+        wa_bf = [round_wa(0, nc.scalar.copy), round_wa(1, nc.vector.tensor_copy)]
+        res_t = sbuf("res_t", [P, 4, D], F32, "wa_raw")
+        load_rows(res_t, res)
+        wa_q = [quantise("wa_q%d" % h, wa_bf[h]) for h in range(2)]
+        z_wv = sbuf("z_wv", [P, D + H, 4], BF16)
+        wb_bf = [round_wb(h, nc.scalar.copy) for h in range(2)]
+        wb_q = [quantise("wb_q%d" % h, wb_bf[h]) for h in range(2)]
+        place = (1, 2, 0, 3)
+        for t in range(4):
+            direct_bank(z_wv[:, cols(1 + place[t])], t % 2, x_tile, whole(wa_q[t // 2]), t, g_t)
+        z2_pl = [planes("z2%d" % h, x_tile, whole(wb_q[h]), (4 + 2 * h, 5 + 2 * h), g_i) for h in range(2)]
+        z2_wv = weave("z20", z2_pl[0])
+        z_c = sbuf("z_c", [P, D], U32)
+        z_s = sbuf("z_s", [P, D], U8)
+        nc.vector.quantize_mx(out=z_c[:].bitcast(FP8X4), scales=z_s[:], in_=flat(z_wv[:, P : P + D]))
+        z2_q = [quantise("z2_q0", z2_wv), quantise("z2_q1", weave("z21", z2_pl[1]))]
+
+        def z_tile(t):
+            return z_c[:, cols(place[t])].bitcast(FP8X4), z_s[:, cols(place[t])]
+
+        deal(w1s_d[:], w1s[:])
+        deal(w1w_d[:], w1w[:])
+        y_pl = [planes("y0", w1_tile, q_half(0), (0, 1), g_q)]
+        c_pl = [planes("c0", z_tile, whole(z2_q[0]), (2, 3), g_k)]
+        y_pl.append(planes("y1", w1_tile, q_half(1), (4, 5), g_q))
+        c_pl.append(planes("c1", z_tile, whole(z2_q[1]), (6, 7), g_k))
+        z4_c = sbuf("z4_c", [P, D], U32)
+        z4_s = sbuf("z4_s", [P, D], U8)
+        z3_wv = [weave("z30", c_pl[0])]
         for h in range(2):
-            wb_bf = sbuf("wb_bf%d" % h, [P, 4, 64, 4], BF16, slot="wb_bf")
-            cast = nc.vector.tensor_copy if h else nc.scalar.copy
-            cast(wb_bf[:].rearrange("p t m j -> p m j t"), wb_raw[h][:].rearrange("p j (m t) -> p m j t", t=4))
-            wb_q.append(quantise("wb_q%d" % h, flat(wb_bf[:]), 256))
-        w1w_d = sbuf("w1w_d", [P, 2 * D], U8, slot="wb_bf")
-        z_wv = [sbuf("z_wv0", [P, 2, P, 4], BF16), sbuf("z_wv1", [P, 2, P, 4], BF16, slot="wb_raw1")]
-        direct(lambda u: z_wv[u][:, :, 64:128], x_tile, wa_q[1], (0, 1), g_t)
-        deal(w1w_d, w1w)
-        z_pl = project("z0", x_tile, whole(wa_q[0]), (2, 3), g_t)
-        z2_pl = [project("z2%d" % h, x_tile, whole(wb_q[h]), (4 + 2 * h, 5 + 2 * h), g_i) for h in range(2)]
-        gate_ps = bank(0)
-        nc.tensor.transpose(gate_ps[:, 0:P], gate_rows[:], ident[:])
-        g_q = sbuf("g_q", [P, 4], F32)
-        g_k = sbuf("g_k", [P, 4], F32)
-        nc.scalar.copy(g_q[:], gate_ps[:, 0:4])
-        nc.scalar.activation(g_k[:], gate_ps[:, 4:8], COPY, scale=0.0625)
-        for u in range(2):
-            weave_pair(z_wv[u][:, :, 0:64], z_pl, u)
-        w1s_d = sbuf("w1s_d", [P, D], U8, slot="z0_pl")
-        deal(w1s_d, w1s)
-        y_pl = project("y0", w1_tile, q_cols(0, 256), (0, 1), g_q)
-        z2_wv0 = woven_half("z20", z2_pl[0])
-        z_q = [quantise("z_q%d" % h, flat(z_wv[h][:]), 256) for h in range(2)]
-        z2_q = [quantise("z2_q0", z2_wv0, 256), quantise("z2_q1", woven_half("z21", z2_pl[1]), 256)]
-        c_pl = [project("c%d" % h, halves(z_q), whole(z2_q[h]), (2 + 2 * h, 3 + 2 * h), g_k) for h in range(2)]
-        weave(z3_wv[:, :, 0:64], c_pl[0])
-        for u in range(2):
-            nc.vector.tensor_copy(
-                z3_wv[:, 2 * u : 2 * u + 2, 64:128].rearrange("p e (c i) t -> p e c t i", i=4),
-                c_pl[1][:, :, cols(u)].rearrange("p t (e c i) -> p e c t i", e=2, i=4),
+            nc.vector.quantize_mx(
+                out=z4_c[:, cols(h, H)].bitcast(FP8X4), scales=z4_s[:, cols(h, H)],
+                in_=flat(weave("z4%d" % h, y_pl[h])[:]),
             )
-        z3_q = [quantise("z3_q%d" % h, flat(z3_wv[:, 2 * h : 2 * h + 2]), 256) for h in range(2)]
-        z4_q = [quantise("z4_q0", woven_half("z40", y_pl), 256)]
-        y_pl = project("y1", w1_tile, q_cols(256, 256), (6, 7), g_q)
-        z4_q.append(quantise("z4_q1", woven_half("z41", y_pl), 256))
+        z3_q = [quantise("z3_q0", z3_wv[0]), quantise("z3_q1", weave("z31", c_pl[1]))]
 
         out_v = out_0.rearrange("(p t) v -> p t v", t=4)
         words_v = out_1[0].rearrange("p n t -> p (n t)").bitcast(I32)
         o_s = sbuf("o_s", [P, D], U8)
         o_w = sbuf("o_w", [P, D], U32)
-        o_f = [sbuf("o_f%d" % h, [P, 4, 256], F32) for h in range(2)]
-        o_bf = [sbuf("o_bf%d" % c, [P, P, 4], BF16) for c in range(4)]
-        for h in range(2):
-            v_half = slice(256 * h, 256 * h + 256)
-            for u in range(2):
-                acc = bank(2 + 2 * h + u)
-                rw, rs = whole(z4_q[h])
+        o_f = sbuf("o_f", [P, 4, D], F32)
+        o_bf = [sbuf("o_bf%d" % h, [P, H, 4], BF16) for h in range(2)]
+        for a in range(2):
+            rows = slice(2 * a, 2 * a + 2)
+            for h in range(2):
+                acc = bank(2 * a + h)
                 for e in range(2):
-                    lw, ls = halves(z3_q)(2 * u + e)
-                    mm(acc[:, 256 * e : 256 * e + 256], lw, ls, rw, rs)
+                    lw, ls = tiles_of(z3_q)(2 * a + e)
+                    mm(acc[:, cols(e, H)], lw, ls, z4_c[:, cols(h, H)].bitcast(FP8X4), z4_s[:, cols(h, H)])
                 nc.vector.scalar_tensor_tensor(
-                    o_f[h][:, 2 * u : 2 * u + 2], acc[:].rearrange("p (e n) -> p e n", e=2), -0.03125,
-                    res_t[:, 2 * u : 2 * u + 2, v_half], MULT, ADD,
+                    o_f[:, rows, cols(h, H)], acc[:].rearrange("p (e n) -> p e n", e=2), -0.03125,
+                    res_t[:, rows, cols(h, H)], MULT, ADD,
                 )
-                nc.sync.dma_start(out_v[:, 2 * u : 2 * u + 2, v_half], o_f[h][:, 2 * u : 2 * u + 2])
-            for c in (2 * h, 2 * h + 1):
-                cast = nc.vector.tensor_copy if c == 3 else nc.scalar.copy
-                cast(
-                    o_bf[c][:].rearrange("p (c i) t -> p c t i", i=4),
-                    o_f[h][:, :, cols(c % 2)].rearrange("p t (c i) -> p c t i", i=4),
-                )
-        for c in (0, 1, 3, 2):
-            nc.vector.quantize_mx(
-                out=o_w[:, cols(c)].bitcast(FP8X4), scales=o_s[:, cols(c)], in_=o_bf[c][:].rearrange("p n t -> p (n t)")
+                if a:
+                    nc.sync.dma_start(out_v[:, rows, cols(h, H)], o_f[:, rows, cols(h, H)])
+            if not a:
+                nc.sync.dma_start(out_v[:, rows], o_f[:, rows])
+        for c in range(4):
+            cast = nc.vector.tensor_copy if c % 2 else nc.scalar.copy
+            cast(
+                o_bf[c // 2][:, cols(c % 2)].rearrange("p (c i) t -> p c t i", i=4),
+                o_f[:, :, cols(c)].rearrange("p t (c i) -> p c t i", i=4),
             )
-            if c in (1, 2):
-                v_half = slice(256 * (c // 2), 256 * (c // 2) + 256)
-                nc.sync.dma_start(words_v[:, v_half], o_w[:, v_half].bitcast(I32))
+        for h in range(2):
+            nc.vector.quantize_mx(out=o_w[:, cols(h, H)].bitcast(FP8X4), scales=o_s[:, cols(h, H)], in_=flat(o_bf[h][:]))
+            nc.sync.dma_start(words_v[:, cols(h, H)], o_w[:, cols(h, H)].bitcast(I32))
         for q in range(4):
             eng = nc.scalar if q % 2 else nc.sync
             eng.dma_start(out_2[0, 4 * q : 4 * q + 4, :].bitcast(I32), o_s[32 * q : 32 * q + 4, :].bitcast(I32))

@@ -48,23 +48,23 @@ def tile_picked_decorr_none_po_kernel(
         gate_rows = sbuf("gate_rows", [P, D], F32)
         ident = sbuf("ident", [P, P], F32)
         picked_s = sbuf("picked_s", [P, 2 * D], U8)
-        plane_s = sbuf("plane_s", [P, 2 * D], U8)
+        w1s = sbuf("w1s", [P, D], U8)
+        rows_s = sbuf("rows_s", [P, 3 * D], U8)
+        plane_s = sbuf("plane_s", [P, 3 * D], U8)
 
         nc.gpsimd.memset(xs[0 : P - 16, :].bitcast(I32), 0)
-        nc.vector.memset(gate_rows[0 : P - 4, :], 0.0)
+        nc.vector.memset(w1s[0 : P - 16, :].bitcast(I32), 0)
+        nc.vector.memset(gate_rows[96 : P - 4, :], 0.0)
         nc.vector.memset(plane_s[:].bitcast(I32), 0)
         make_identity(nc, ident[:])
-
-        def load_scales(dst, src, quads):
-            for q in quads:
-                nc.sync.dma_start(dst[32 * q : 32 * q + 4, :].bitcast(I32), src[0, 4 * q : 4 * q + 4, :].bitcast(I32))
 
         def load_rows(dst, w):
             nc.sync.dma_start(dst[:], w.rearrange("(p j) c -> p j c", j=4))
 
-        nc.sync.dma_start(xs[P - 16 : P, :].bitcast(I32), x_scales[0].bitcast(I32))
         nc.sync.dma_start(offs_t[:], offs)
         nc.sync.dma_start(qs_t[:], qs)
+        nc.sync.dma_start(xs[P - 16 : P, :].bitcast(I32), x_scales[0].bitcast(I32))
+        nc.sync.dma_start(w1s[P - 16 : P, :].bitcast(I32), w1_scales[0].bitcast(I32))
         nc.sync.dma_start(xw[:], x_words[0].rearrange("p n t -> p (n t)").bitcast(I32))
         for g, gate in enumerate((gt, gi, gq, gk)):
             nc.sync.dma_start(gate_rows[P - 4 + g : P - 3 + g, :], gate.rearrange("n o -> o n"))
@@ -72,8 +72,10 @@ def tile_picked_decorr_none_po_kernel(
         nc.sync.dma_start(w1w[:].bitcast(I32), w1_words[0].bitcast(I32))
 
         gate_dealt = sbuf("gate_dealt", [P, 4, P], F32)
+        nc.scalar.activation(gate_dealt[0:96], ident[0:96].unsqueeze(1).to_broadcast([96, 4, P]), COPY, scale=0.0)
         nc.scalar.copy(
-            gate_dealt[:].rearrange("g t (u r) -> g t u r", r=4), gate_rows[:].rearrange("g (u t r) -> g t u r", t=4, r=4)
+            gate_dealt[96:P].rearrange("g t (u r) -> g t u r", r=4),
+            gate_rows[96:P].rearrange("g (u t r) -> g t u r", t=4, r=4),
         )
         gate_ps = bank(7)
         for t in range(4):
@@ -138,36 +140,34 @@ def tile_picked_decorr_none_po_kernel(
                 src.bitcast(I32).rearrange("p (u t w) -> p t u w", t=4, u=32),
             )
 
-        a_s = sbuf("a_s", [P, D], U8)
         a_w = sbuf("a_w", [P, D], U32)
-        q_w = sbuf("q_w", [P, D], U32)
         w1w_d = sbuf("w1w_d", [P, 2 * D], U8)
-        w1s_d = sbuf("w1s_d", [P, D], U8)
         nc.vector.tensor_copy(picked_s[:, 0:D], xs[:].indirect(offs_t[:]))
         nc.vector.tensor_copy(picked_s[:, D : 2 * D], xs[:].indirect(qs_t[:]))
+        deal(rows_s[:, cols(0, D)], picked_s[:, 0:D])
+        deal(rows_s[:, cols(2, D)], w1s[:])
+        nc.vector.tensor_copy(rows_s[:, cols(1, D)].bitcast(I32), picked_s[:, cols(1, D)].bitcast(I32))
         for q in range(4):
             nc.sync.dma_start(
-                plane_s[32 * q : 32 * q + 4, :].bitcast(I32), picked_s[P - 16 + 4 * q : P - 12 + 4 * q, :].bitcast(I32)
+                plane_s[32 * q : 32 * q + 4, :].bitcast(I32), rows_s[P - 16 + 4 * q : P - 12 + 4 * q, :].bitcast(I32)
             )
-        wb_raw = sbuf("wb_raw", [P, 4, D], F32, "xs")
+        wb_raw = sbuf("wb_raw", [P, 4, D], F32, "picked_s")
         load_rows(wb_raw, wb)
         nc.vector.tensor_copy(
             a_w[:].rearrange("p (t u r) -> p u t r", t=4, r=4), xw[:].bitcast(U32).indirect(offs_t[:])
         )
-        nc.vector.tensor_copy(q_w[:], xw[:].bitcast(U32).indirect(qs_t[:]))
-        deal(a_s[:], plane_s[:, 0:D])
-        w1s = sbuf("w1s", [P, D], U8, "xw")
-        nc.gpsimd.memset(w1s[:].bitcast(I32), 0)
-        load_scales(w1s, w1_scales, range(4))
+        q_w = [sbuf("q_w0", [P, H], U32)]
+        nc.vector.tensor_copy(q_w[0][:], xw[:].bitcast(U32).indirect(qs_t[:, cols(0, 16)]))
+        deal(w1w_d[:], w1w[:])
 
         def x_tile(t):
-            return a_w[:, cols(t)].bitcast(FP8X4), a_s[:, cols(t)]
+            return a_w[:, cols(t)].bitcast(FP8X4), plane_s[:, cols(t)]
 
         def w1_tile(t):
-            return w1w_d[:, cols(t, H)].bitcast(FP4X4), w1s_d[:, cols(t)]
+            return w1w_d[:, cols(t, H)].bitcast(FP4X4), plane_s[:, cols(8 + t)]
 
         def q_half(h):
-            return q_w[:, cols(h, H)], plane_s[:, cols(2 + h, H)]
+            return q_w[h][:], plane_s[:, cols(2 + h, H)]
 
         def round_wa(h, cast, slot=None):
             dst = sbuf("wa_bf%d" % h, [P, H, 4], BF16, slot)
@@ -185,20 +185,20 @@ def tile_picked_decorr_none_po_kernel(
             )
             return dst
 
-        warm = bank(6)
-        for r in range(3):
-            mm(warm[:], q_w[:, cols(r)].bitcast(FP8X4), plane_s[:, cols(4 + r)], q_w[:].bitcast(FP8X4), plane_s[:, cols(1, D)])
-        wa_bf = [round_wa(0, nc.scalar.copy), round_wa(1, nc.vector.tensor_copy)]
+        wa_bf = [round_wa(0, nc.vector.tensor_copy), round_wa(1, nc.scalar.copy)]
         res_t = sbuf("res_t", [P, 4, D], F32, "wa_raw")
         load_rows(res_t, res)
+        y_pl = [planes("y0", w1_tile, q_half(0), (4, 5), g_q)]
         wa_q = [quantise("wa_q%d" % h, wa_bf[h]) for h in range(2)]
+        q_w.append(sbuf("q_w1", [P, H], U32, "wa_bf0"))
+        nc.vector.tensor_copy(q_w[1][:], xw[:].bitcast(U32).indirect(qs_t[:, cols(1, 16)]))
         z_wv = sbuf("z_wv", [P, D + H, 4], BF16)
         wb_bf = [round_wb(h, nc.scalar.copy) for h in range(2)]
         wb_q = [quantise("wb_q%d" % h, wb_bf[h]) for h in range(2)]
         place = (1, 2, 0, 3)
         for t in range(4):
             direct_bank(z_wv[:, cols(1 + place[t])], t % 2, x_tile, whole(wa_q[t // 2]), t, g_t)
-        z2_pl = [planes("z2%d" % h, x_tile, whole(wb_q[h]), (4 + 2 * h, 5 + 2 * h), g_i) for h in range(2)]
+        z2_pl = [planes("z2%d" % h, x_tile, whole(wb_q[h]), (6 - 2 * h, 7 - 2 * h), g_i) for h in range(2)]
         z2_wv = weave("z20", z2_pl[0])
         z_c = sbuf("z_c", [P, D], U32)
         z_s = sbuf("z_s", [P, D], U8)
@@ -208,19 +208,15 @@ def tile_picked_decorr_none_po_kernel(
         def z_tile(t):
             return z_c[:, cols(place[t])].bitcast(FP8X4), z_s[:, cols(place[t])]
 
-        deal(w1s_d[:], w1s[:])
-        deal(w1w_d[:], w1w[:])
-        y_pl = [planes("y0", w1_tile, q_half(0), (0, 1), g_q)]
-        c_pl = [planes("c0", z_tile, whole(z2_q[0]), (2, 3), g_k)]
-        y_pl.append(planes("y1", w1_tile, q_half(1), (4, 5), g_q))
-        c_pl.append(planes("c1", z_tile, whole(z2_q[1]), (6, 7), g_k))
-        z4_c = sbuf("z4_c", [P, D], U32)
+        y_pl.append(planes("y1", w1_tile, q_half(1), (6, 7), g_q))
+        c_pl = [planes("c%d" % h, z_tile, whole(z2_q[h]), (6 * h, 6 * h + 1), g_k) for h in range(2)]
+        z4_c = sbuf("z4_c", [P, D], U32, "z_wv")
         z4_s = sbuf("z4_s", [P, D], U8)
         z3_wv = [weave("z30", c_pl[0])]
         for h in range(2):
             nc.vector.quantize_mx(
                 out=z4_c[:, cols(h, H)].bitcast(FP8X4), scales=z4_s[:, cols(h, H)],
-                in_=flat(weave("z4%d" % h, y_pl[h])[:]),
+                in_=flat(weave("z4%d" % h, y_pl[h], "z21_wv" if h else None)[:]),
             )
         z3_q = [quantise("z3_q0", z3_wv[0]), quantise("z3_q1", weave("z31", c_pl[1]))]
 
@@ -230,21 +226,22 @@ def tile_picked_decorr_none_po_kernel(
         o_w = sbuf("o_w", [P, D], U32)
         o_f = sbuf("o_f", [P, 4, D], F32)
         o_bf = [sbuf("o_bf%d" % h, [P, H, 4], BF16) for h in range(2)]
-        for a in range(2):
-            rows = slice(2 * a, 2 * a + 2)
-            for h in range(2):
-                acc = bank(2 * a + h)
-                for e in range(2):
-                    lw, ls = tiles_of(z3_q)(2 * a + e)
-                    mm(acc[:, cols(e, H)], lw, ls, z4_c[:, cols(h, H)].bitcast(FP8X4), z4_s[:, cols(h, H)])
-                nc.vector.scalar_tensor_tensor(
-                    o_f[:, rows, cols(h, H)], acc[:].rearrange("p (e n) -> p e n", e=2), -0.03125,
-                    res_t[:, rows, cols(h, H)], MULT, ADD,
-                )
-                if a:
-                    nc.sync.dma_start(out_v[:, rows, cols(h, H)], o_f[:, rows, cols(h, H)])
-            if not a:
-                nc.sync.dma_start(out_v[:, rows], o_f[:, rows])
+        for t in range(2):
+            acc = bank(2 + t)
+            lw, ls = tiles_of(z3_q)(t)
+            mm(acc[:], lw, ls, z4_c[:].bitcast(FP8X4), z4_s[:])
+            nc.vector.scalar_tensor_tensor(o_f[:, t], acc[:], -0.03125, res_t[:, t], MULT, ADD)
+            nc.sync.dma_start(out_v[:, t], o_f[:, t])
+        for h in range(2):
+            acc = bank(4 + h)
+            for e in range(2):
+                lw, ls = tiles_of(z3_q)(2 + e)
+                mm(acc[:, cols(e, H)], lw, ls, z4_c[:, cols(h, H)].bitcast(FP8X4), z4_s[:, cols(h, H)])
+            nc.vector.scalar_tensor_tensor(
+                o_f[:, 2:4, cols(h, H)], acc[:].rearrange("p (e n) -> p e n", e=2), -0.03125,
+                res_t[:, 2:4, cols(h, H)], MULT, ADD,
+            )
+            nc.sync.dma_start(out_v[:, 2:4, cols(h, H)], o_f[:, 2:4, cols(h, H)])
         for c in range(4):
             cast = nc.vector.tensor_copy if c % 2 else nc.scalar.copy
             cast(

@@ -28,10 +28,14 @@ def tile_picked_decorr_none_po_kernel(
     nc = tc.nc
     with ExitStack() as ctx:
         sb = ctx.enter_context(tc.tile_pool(name="sb", bufs=1))
+        shared = ctx.enter_context(tc.tile_pool(name="shared", bufs=1))
         ps = ctx.enter_context(tc.psum_pool(name="ps", bufs=1))
 
         def sbuf(name, shape, dtype, slot=None):
             return sb.tile(shape, dtype, name=name, tag=slot or name, align_bytes=64)
+
+        def placed(name, shape, dtype, offset):
+            return shared.tile(shape, dtype, name=name, align_bytes=64, offset=offset)
 
         def bank(b):
             return ps.tile([P, D], F32, name="bank%d" % b)
@@ -47,7 +51,7 @@ def tile_picked_decorr_none_po_kernel(
         w1w = sbuf("w1w", [P, 2 * D], U8)
         gate_rows = sbuf("gate_rows", [P, D], F32)
         ident = sbuf("ident", [P, P], F32)
-        picked_s = sbuf("picked_s", [P, 2 * D], U8)
+        picked_s = placed("picked_s", [P, 2 * D], U8, 0)
         w1s = sbuf("w1s", [P, D], U8)
         rows_s = sbuf("rows_s", [P, 3 * D], U8)
         plane_s = sbuf("plane_s", [P, 3 * D], U8)
@@ -80,18 +84,22 @@ def tile_picked_decorr_none_po_kernel(
         gate_ps = bank(7)
         for t in range(4):
             nc.tensor.transpose(gate_ps[:, cols(t)], gate_dealt[:, t], ident[:])
-        gates = sbuf("gates", [P, 3, 4], F32)
-        g_k = sbuf("g_k", [P, 4], F32)
         turned = gate_ps[:].rearrange("p (t g) -> p g t", t=4)
-        nc.scalar.copy(gates[:], turned[:, P - 4 : P - 1])
-        nc.scalar.activation(g_k[:], turned[:, P - 1], COPY, scale=0.0625)
-        g_t, g_i, g_q = gates[:, 0], gates[:, 1], gates[:, 2]
+
+        def gate(name, g, factor=1.0):
+            tile = sbuf(name, [P, 4], F32)
+            nc.scalar.activation(tile[:], turned[:, P - 4 + g], COPY, scale=factor)
+            return tile[:]
+
+        g_t, g_q = gate("g_t", 0), gate("g_q", 2)
+        g_i = [gate("g_i%d" % h, 1) for h in range(2)]
+        g_k = [gate("g_k%d" % h, 3, 0.0625) for h in range(2)]
 
         def flat(ap):
             return ap.rearrange("p n t -> p (n t)")
 
-        def quantise(name, woven, slot=None):
-            codes = sbuf(name + "_c", [P, H], U32, slot)
+        def quantise(name, woven, slot=None, offset=None):
+            codes = sbuf(name + "_c", [P, H], U32, slot) if offset is None else placed(name + "_c", [P, H], U32, offset)
             scales = sbuf(name + "_s", [P, H], U8)
             nc.vector.quantize_mx(out=codes[:].bitcast(FP8X4), scales=scales[:], in_=flat(woven[:]))
             return codes, scales
@@ -101,18 +109,19 @@ def tile_picked_decorr_none_po_kernel(
 
         def planes(name, stationary, moving, banks, gate):
             pl = sbuf(name + "_pl", [P, 4, H], BF16)
-            for u in range(2):
-                acc = bank(banks[u])
-                for e in range(2):
-                    lw, ls = stationary(2 * u + e)
-                    mm(acc[:, cols(e, H)], lw, ls, moving[0].bitcast(FP8X4), moving[1])
-                for e in range(2):
-                    t = 2 * u + e
-                    nc.scalar.activation(pl[:, t, :], acc[:, cols(e, H)], COPY, scale=gate[:, t : t + 1])
+            per_bank = 4 // len(banks)
+            for u, b in enumerate(banks):
+                acc = bank(b)
+                tiles = range(per_bank * u, per_bank * (u + 1))
+                for t in tiles:
+                    lw, ls = stationary(t)
+                    mm(acc[:, cols(t % per_bank, H)], lw, ls, moving[0].bitcast(FP8X4), moving[1])
+                for t in tiles:
+                    nc.scalar.activation(pl[:, t, :], acc[:, cols(t % per_bank, H)], COPY, scale=gate[:, t : t + 1])
             return pl
 
-        def weave(name, pl, slot=None):
-            woven = sbuf(name + "_wv", [P, H, 4], BF16, slot)
+        def weave(name, pl, offset=None):
+            woven = sbuf(name + "_wv", [P, H, 4], BF16) if offset is None else placed(name + "_wv", [P, H, 4], BF16, offset)
             nc.vector.tensor_copy(
                 woven[:].rearrange("p (c i) t -> p c t i", i=4), pl[:].rearrange("p t (c i) -> p c t i", i=4)
             )
@@ -151,7 +160,7 @@ def tile_picked_decorr_none_po_kernel(
             nc.sync.dma_start(
                 plane_s[32 * q : 32 * q + 4, :].bitcast(I32), rows_s[P - 16 + 4 * q : P - 12 + 4 * q, :].bitcast(I32)
             )
-        wb_raw = sbuf("wb_raw", [P, 4, D], F32, "picked_s")
+        wb_raw = placed("wb_raw", [P, 4, D], F32, 0)
         load_rows(wb_raw, wb)
         nc.vector.tensor_copy(
             a_w[:].rearrange("p (t u r) -> p u t r", t=4, r=4), xw[:].bitcast(U32).indirect(offs_t[:])
@@ -178,7 +187,7 @@ def tile_picked_decorr_none_po_kernel(
             return dst
 
         def round_wb(h, cast):
-            dst = z_wv[:, cols(2 * h, H)]
+            dst = sbuf("wb_bf1", [P, H, 4], BF16)[:] if h else z_wv[:, D - P : D + P]
             cast(
                 dst.rearrange("p (t m) j -> p m j t", t=2),
                 wb_raw[:].rearrange("p j (m t) -> p m j t", t=4)[:, :, :, 2 * h : 2 * h + 2],
@@ -188,37 +197,31 @@ def tile_picked_decorr_none_po_kernel(
         wa_bf = [round_wa(0, nc.vector.tensor_copy), round_wa(1, nc.scalar.copy)]
         res_t = sbuf("res_t", [P, 4, D], F32, "wa_raw")
         load_rows(res_t, res)
-        y_pl = [planes("y0", w1_tile, q_half(0), (4, 5), g_q)]
+        y_pl = [planes("y0", w1_tile, q_half(0), (4, 5, 6, 7), g_q)]
         wa_q = [quantise("wa_q%d" % h, wa_bf[h]) for h in range(2)]
         q_w.append(sbuf("q_w1", [P, H], U32, "wa_bf0"))
         nc.vector.tensor_copy(q_w[1][:], xw[:].bitcast(U32).indirect(qs_t[:, cols(1, 16)]))
-        z_wv = sbuf("z_wv", [P, D + H, 4], BF16)
+        z_wv = sbuf("z_wv", [P, D + P, 4], BF16)
         wb_bf = [round_wb(h, nc.scalar.copy) for h in range(2)]
         wb_q = [quantise("wb_q%d" % h, wb_bf[h]) for h in range(2)]
-        place = (1, 2, 0, 3)
         for t in range(4):
-            direct_bank(z_wv[:, cols(1 + place[t])], t % 2, x_tile, whole(wa_q[t // 2]), t, g_t)
-        z2_pl = [planes("z2%d" % h, x_tile, whole(wb_q[h]), (6 - 2 * h, 7 - 2 * h), g_i) for h in range(2)]
+            direct_bank(z_wv[:, cols(t)], t % 2, x_tile, whole(wa_q[t // 2]), t, g_t)
+        z2_pl = [planes("z2%d" % h, x_tile, whole(wb_q[h]), ((0, 1, 6, 7), (4, 5))[h], g_i[h]) for h in range(2)]
+        z4_wv = weave("z40", y_pl[0], 0)
+        z_q = [quantise("z_q0", z_wv[:, cols(0, H)], offset=8 * H)]
         z2_wv = weave("z20", z2_pl[0])
-        z_c = sbuf("z_c", [P, D], U32)
-        z_s = sbuf("z_s", [P, D], U8)
-        nc.vector.quantize_mx(out=z_c[:].bitcast(FP8X4), scales=z_s[:], in_=flat(z_wv[:, P : P + D]))
-        z2_q = [quantise("z2_q0", z2_wv), quantise("z2_q1", weave("z21", z2_pl[1]))]
-
-        def z_tile(t):
-            return z_c[:, cols(place[t])].bitcast(FP8X4), z_s[:, cols(place[t])]
-
+        z_q.append(quantise("z_q1", z_wv[:, cols(1, H)], "g_i0"))
+        z2_q = [quantise("z2_q0", z2_wv)]
+        z2_wv = weave("z21", z2_pl[1])
+        z4_q = [quantise("z4_q0", z4_wv, "g_i1")]
+        z2_q.append(quantise("z2_q1", z2_wv))
         y_pl.append(planes("y1", w1_tile, q_half(1), (6, 7), g_q))
-        c_pl = [planes("c%d" % h, z_tile, whole(z2_q[h]), (6 * h, 6 * h + 1), g_k) for h in range(2)]
-        z4_c = sbuf("z4_c", [P, D], U32, "z_wv")
-        z4_s = sbuf("z4_s", [P, D], U8)
-        z3_wv = [weave("z30", c_pl[0])]
-        for h in range(2):
-            nc.vector.quantize_mx(
-                out=z4_c[:, cols(h, H)].bitcast(FP8X4), scales=z4_s[:, cols(h, H)],
-                in_=flat(weave("z4%d" % h, y_pl[h], "z21_wv" if h else None)[:]),
-            )
-        z3_q = [quantise("z3_q0", z3_wv[0]), quantise("z3_q1", weave("z31", c_pl[1]))]
+        c_pl = [planes("c%d" % h, tiles_of(z_q), whole(z2_q[h]), (6 * h, 6 * h + 1), g_k[h]) for h in range(2)]
+        z4_wv = weave("z41", y_pl[1])
+        z3_wv = weave("z30", c_pl[0])
+        z4_q.append(quantise("z4_q1", z4_wv, "g_k0"))
+        z3_q = [quantise("z3_q0", z3_wv)]
+        z3_wv = weave("z31", c_pl[1])
 
         out_v = out_0.rearrange("(p t) v -> p t v", t=4)
         words_v = out_1[0].rearrange("p n t -> p (n t)").bitcast(I32)
@@ -226,17 +229,23 @@ def tile_picked_decorr_none_po_kernel(
         o_w = sbuf("o_w", [P, D], U32)
         o_f = sbuf("o_f", [P, 4, D], F32)
         o_bf = [sbuf("o_bf%d" % h, [P, H, 4], BF16) for h in range(2)]
+        accs = []
         for t in range(2):
-            acc = bank(2 + t)
+            accs.append(bank(2 + t))
             lw, ls = tiles_of(z3_q)(t)
-            mm(acc[:], lw, ls, z4_c[:].bitcast(FP8X4), z4_s[:])
+            for h in range(2):
+                mm(accs[t][:, cols(h, H)], lw, ls, z4_q[h][0][:].bitcast(FP8X4), z4_q[h][1][:])
+        for t in range(2):
+            acc = accs[t]
             nc.vector.scalar_tensor_tensor(o_f[:, t], acc[:], -0.03125, res_t[:, t], MULT, ADD)
             nc.sync.dma_start(out_v[:, t], o_f[:, t])
+            if t == 0:
+                z3_q.append(quantise("z3_q1", z3_wv, "z3_q0_c"))
         for h in range(2):
             acc = bank(4 + h)
             for e in range(2):
                 lw, ls = tiles_of(z3_q)(2 + e)
-                mm(acc[:, cols(e, H)], lw, ls, z4_c[:, cols(h, H)].bitcast(FP8X4), z4_s[:, cols(h, H)])
+                mm(acc[:, cols(e, H)], lw, ls, z4_q[h][0][:].bitcast(FP8X4), z4_q[h][1][:])
             nc.vector.scalar_tensor_tensor(
                 o_f[:, 2:4, cols(h, H)], acc[:].rearrange("p (e n) -> p e n", e=2), -0.03125,
                 res_t[:, 2:4, cols(h, H)], MULT, ADD,

@@ -194,6 +194,9 @@ def tile_picked_decorr_none_po_kernel(
             )
             return dst
 
+        warm = bank(3)
+        for r in range(2):
+            mm(warm[:], a_w[:, cols(r)].bitcast(FP8X4), rows_s[:, cols(r)], a_w[:].bitcast(FP8X4), rows_s[:, cols(0, D)])
         wa_bf = [round_wa(0, nc.vector.tensor_copy), round_wa(1, nc.scalar.copy)]
         res_t = sbuf("res_t", [P, 4, D], F32, "wa_raw")
         load_rows(res_t, res)
@@ -217,6 +220,9 @@ def tile_picked_decorr_none_po_kernel(
         z2_q.append(quantise("z2_q1", z2_wv))
         y_pl.append(planes("y1", w1_tile, q_half(1), (6, 7), g_q))
         c_pl = [planes("c%d" % h, tiles_of(z_q), whole(z2_q[h]), (6 * h, 6 * h + 1), g_k[h]) for h in range(2)]
+        warm = bank(1)
+        for r in range(2):
+            mm(warm[:], a_w[:, cols(r)].bitcast(FP8X4), rows_s[:, cols(r)], a_w[:].bitcast(FP8X4), rows_s[:, cols(0, D)])
         z4_wv = weave("z41", y_pl[1])
         z3_wv = weave("z30", c_pl[0])
         z4_q.append(quantise("z4_q1", z4_wv, "g_k0"))

@@ -133,8 +133,8 @@ def tile_picked_decorr_none_po_kernel(
                 lw, ls = stationary(t)
                 mm(acc[:, cols(t)], lw, ls, moving[0][:, cols(u)].bitcast(FP8X4), moving[1][:, cols(u)])
             nc.vector.tensor_tensor(
-                dst, acc[:].rearrange("p (t n) -> p n t", t=4),
-                gate.unsqueeze(1).to_broadcast([P, P, 4]), MULT,
+                dst.rearrange("p (c i) t -> p c t i", i=2), acc[:].rearrange("p (t c i) -> p c t i", t=4, i=2),
+                gate.unsqueeze(1).unsqueeze(3).to_broadcast([P, P // 2, 4, 2]), MULT,
             )
 
         def whole(q):
@@ -210,7 +210,8 @@ def tile_picked_decorr_none_po_kernel(
         for t in range(4):
             direct_bank(z_wv[:, cols(t)], t % 2, x_tile, whole(wa_q[t // 2]), t, g_t)
         z2_pl = [planes("z2%d" % h, x_tile, whole(wb_q[h]), ((0, 1, 6, 7), (4, 5))[h], g_i[h]) for h in range(2)]
-        z4_wv = weave("z40", y_pl[0], 0)
+        z4_wv = sbuf("z40_wv", [P, H, 4], BF16)
+        nc.gpsimd.tensor_scalar(z4_wv[:], y_pl[0][:].rearrange("p t n -> p n t"), 1.0, 0.0, MULT, ADD)
         z_q = [quantise("z_q0", z_wv[:, cols(0, H)], offset=8 * H)]
         z2_wv = weave("z20", z2_pl[0])
         z_q.append(quantise("z_q1", z_wv[:, cols(1, H)], "g_i0"))
@@ -235,18 +236,21 @@ def tile_picked_decorr_none_po_kernel(
         o_w = sbuf("o_w", [P, D], U32)
         o_f = sbuf("o_f", [P, 4, D], F32)
         o_bf = [sbuf("o_bf%d" % h, [P, H, 4], BF16) for h in range(2)]
-        accs = []
+        z3_q.append(quantise("z3_q1", z3_wv))
+        accs = [bank(2 + t) for t in range(2)]
         for t in range(2):
-            accs.append(bank(2 + t))
-            lw, ls = tiles_of(z3_q)(t)
             for h in range(2):
+                lw, ls = tiles_of(z3_q)(t)
                 mm(accs[t][:, cols(h, H)], lw, ls, z4_q[h][0][:].bitcast(FP8X4), z4_q[h][1][:])
         for t in range(2):
             acc = accs[t]
-            nc.vector.scalar_tensor_tensor(o_f[:, t], acc[:], -0.03125, res_t[:, t], MULT, ADD)
+            if t:
+                nc.vector.scalar_tensor_tensor(o_f[:, t], acc[:], -0.03125, res_t[:, t], MULT, ADD)
+            else:
+                scaled = sbuf("scaled", [P, D], F32)
+                nc.scalar.activation(scaled[:], acc[:], COPY, scale=-0.03125)
+                nc.gpsimd.tensor_tensor(o_f[:, t], scaled[:], res_t[:, t], ADD)
             nc.sync.dma_start(out_v[:, t], o_f[:, t])
-            if t == 0:
-                z3_q.append(quantise("z3_q1", z3_wv, "z3_q0_c"))
         for h in range(2):
             acc = bank(4 + h)
             for e in range(2):

@@ -19,6 +19,11 @@ P = 128
 D = 512
 H = 256
 T = 2048
+ROWS16 = P - 16
+ROWS4 = P - 4
+QUAD3 = 96
+WARM_PASSES = 2
+OUT_FACTOR = -0.03125
 FLOPS = 5 * 2 * D * D * D
 
 
@@ -31,11 +36,11 @@ def tile_picked_decorr_none_po_kernel(
         shared = ctx.enter_context(tc.tile_pool(name="shared", bufs=1))
         ps = ctx.enter_context(tc.psum_pool(name="ps", bufs=1))
 
-        def sbuf(name, shape, dtype, slot=None):
-            return sb.tile(shape, dtype, name=name, tag=slot or name, align_bytes=64)
+        def sbuf(name, shape, dtype, after=None):
+            return sb.tile(shape, dtype, name=name, tag=after or name, align_bytes=64)
 
-        def placed(name, shape, dtype, offset):
-            return shared.tile(shape, dtype, name=name, align_bytes=64, offset=offset)
+        def in_turn(name, shape, dtype):
+            return shared.tile(shape, dtype, name=name, align_bytes=64, offset=0)
 
         def bank(b):
             return ps.tile([P, D], F32, name="bank%d" % b)
@@ -51,14 +56,14 @@ def tile_picked_decorr_none_po_kernel(
         w1w = sbuf("w1w", [P, 2 * D], U8)
         gate_rows = sbuf("gate_rows", [P, D], F32)
         ident = sbuf("ident", [P, P], F32)
-        picked_s = placed("picked_s", [P, 2 * D], U8, 0)
+        picked_s = in_turn("picked_s", [P, 2 * D], U8)
         w1s = sbuf("w1s", [P, D], U8)
         rows_s = sbuf("rows_s", [P, 3 * D], U8)
         plane_s = sbuf("plane_s", [P, 3 * D], U8)
 
-        nc.gpsimd.memset(xs[0 : P - 16, :].bitcast(I32), 0)
-        nc.vector.memset(w1s[0 : P - 16, :].bitcast(I32), 0)
-        nc.vector.memset(gate_rows[96 : P - 4, :], 0.0)
+        nc.gpsimd.memset(xs[0:ROWS16, :].bitcast(I32), 0)
+        nc.vector.memset(w1s[0:ROWS16, :].bitcast(I32), 0)
+        nc.vector.memset(gate_rows[QUAD3:ROWS4, :], 0.0)
         nc.vector.memset(plane_s[:].bitcast(I32), 0)
         make_identity(nc, ident[:])
 
@@ -67,39 +72,41 @@ def tile_picked_decorr_none_po_kernel(
 
         nc.sync.dma_start(offs_t[:], offs)
         nc.sync.dma_start(qs_t[:], qs)
-        nc.sync.dma_start(xs[P - 16 : P, :].bitcast(I32), x_scales[0].bitcast(I32))
-        nc.sync.dma_start(w1s[P - 16 : P, :].bitcast(I32), w1_scales[0].bitcast(I32))
+        nc.sync.dma_start(xs[ROWS16:P, :].bitcast(I32), x_scales[0].bitcast(I32))
+        nc.sync.dma_start(w1s[ROWS16:P, :].bitcast(I32), w1_scales[0].bitcast(I32))
         nc.sync.dma_start(xw[:], x_words[0].rearrange("p n t -> p (n t)").bitcast(I32))
-        for g, gate in enumerate((gt, gi, gq, gk)):
-            nc.sync.dma_start(gate_rows[P - 4 + g : P - 3 + g, :], gate.rearrange("n o -> o n"))
+        for g, vector in enumerate((gt, gi, gq, gk)):
+            nc.sync.dma_start(gate_rows[ROWS4 + g : ROWS4 + g + 1, :], vector.rearrange("n o -> o n"))
         load_rows(wa_raw, wa)
         nc.sync.dma_start(w1w[:].bitcast(I32), w1_words[0].bitcast(I32))
 
         gate_dealt = sbuf("gate_dealt", [P, 4, P], F32)
-        nc.scalar.activation(gate_dealt[0:96], ident[0:96].unsqueeze(1).to_broadcast([96, 4, P]), COPY, scale=0.0)
+        nc.scalar.activation(
+            gate_dealt[0:QUAD3], ident[0:QUAD3].unsqueeze(1).to_broadcast([QUAD3, 4, P]), COPY, scale=0.0
+        )
         nc.scalar.copy(
-            gate_dealt[96:P].rearrange("g t (u r) -> g t u r", r=4),
-            gate_rows[96:P].rearrange("g (u t r) -> g t u r", t=4, r=4),
+            gate_dealt[QUAD3:P].rearrange("g t (u r) -> g t u r", r=4),
+            gate_rows[QUAD3:P].rearrange("g (u t r) -> g t u r", t=4, r=4),
         )
         gate_ps = bank(7)
         for t in range(4):
             nc.tensor.transpose(gate_ps[:, cols(t)], gate_dealt[:, t], ident[:])
         turned = gate_ps[:].rearrange("p (t g) -> p g t", t=4)
 
-        def gate(name, g, factor=1.0):
+        def gate_tile(name, g, factor=1.0):
             tile = sbuf(name, [P, 4], F32)
-            nc.scalar.activation(tile[:], turned[:, P - 4 + g], COPY, scale=factor)
+            nc.scalar.activation(tile[:], turned[:, ROWS4 + g], COPY, scale=factor)
             return tile[:]
 
-        g_t, g_q = gate("g_t", 0), gate("g_q", 2)
-        g_i = [gate("g_i%d" % h, 1) for h in range(2)]
-        g_k = [gate("g_k%d" % h, 3, 0.0625) for h in range(2)]
+        g_t, g_q = gate_tile("g_t", 0), gate_tile("g_q", 2)
+        g_i = [gate_tile("g_i%d" % h, 1) for h in range(2)]
+        g_k = [gate_tile("g_k%d" % h, 3, 0.0625) for h in range(2)]
 
         def flat(ap):
             return ap.rearrange("p n t -> p (n t)")
 
-        def quantise(name, woven, slot=None, offset=None):
-            codes = sbuf(name + "_c", [P, H], U32, slot) if offset is None else placed(name + "_c", [P, H], U32, offset)
+        def quantise(name, woven, after=None):
+            codes = sbuf(name + "_c", [P, H], U32, after)
             scales = sbuf(name + "_s", [P, H], U8)
             nc.vector.quantize_mx(out=codes[:].bitcast(FP8X4), scales=scales[:], in_=flat(woven[:]))
             return codes, scales
@@ -107,27 +114,27 @@ def tile_picked_decorr_none_po_kernel(
         def mm(out, lw, ls, rw, rs):
             nc.tensor.matmul_mx(out=out, lhsT=lw, lhsT_scale=ls, rhs=rw, rhs_scale=rs, start=True, stop=True)
 
-        def planes(name, stationary, moving, banks, gate):
-            pl = sbuf(name + "_pl", [P, 4, H], BF16)
+        def gated_tiles(name, stationary, moving, banks, gate):
+            tiles = sbuf(name + "_pl", [P, 4, H], BF16)
             per_bank = 4 // len(banks)
             for u, b in enumerate(banks):
                 acc = bank(b)
-                tiles = range(per_bank * u, per_bank * (u + 1))
-                for t in tiles:
+                places = range(per_bank * u, per_bank * (u + 1))
+                for t in places:
                     lw, ls = stationary(t)
                     mm(acc[:, cols(t % per_bank, H)], lw, ls, moving[0].bitcast(FP8X4), moving[1])
-                for t in tiles:
-                    nc.scalar.activation(pl[:, t, :], acc[:, cols(t % per_bank, H)], COPY, scale=gate[:, t : t + 1])
-            return pl
+                for t in places:
+                    nc.scalar.activation(tiles[:, t, :], acc[:, cols(t % per_bank, H)], COPY, scale=gate[:, t : t + 1])
+            return tiles
 
-        def weave(name, pl, offset=None):
-            woven = sbuf(name + "_wv", [P, H, 4], BF16) if offset is None else placed(name + "_wv", [P, H, 4], BF16, offset)
+        def weave(name, tiles):
+            woven = sbuf(name + "_wv", [P, H, 4], BF16)
             nc.vector.tensor_copy(
-                woven[:].rearrange("p (c i) t -> p c t i", i=4), pl[:].rearrange("p t (c i) -> p c t i", i=4)
+                woven[:].rearrange("p (c i) t -> p c t i", i=4), tiles[:].rearrange("p t (c i) -> p c t i", i=4)
             )
             return woven
 
-        def direct_bank(dst, u, stationary, moving, b, gate):
+        def gated_woven(dst, u, stationary, moving, b, gate):
             acc = bank(b)
             for t in range(4):
                 lw, ls = stationary(t)
@@ -149,6 +156,11 @@ def tile_picked_decorr_none_po_kernel(
                 src.bitcast(I32).rearrange("p (u t w) -> p t u w", t=4, u=32),
             )
 
+        def warm_up(b):
+            acc = bank(b)
+            for r in range(WARM_PASSES):
+                mm(acc[:], a_w[:, cols(r)].bitcast(FP8X4), rows_s[:, cols(r)], a_w[:].bitcast(FP8X4), rows_s[:, cols(0, D)])
+
         a_w = sbuf("a_w", [P, D], U32)
         w1w_d = sbuf("w1w_d", [P, 2 * D], U8)
         nc.vector.tensor_copy(picked_s[:, 0:D], xs[:].indirect(offs_t[:]))
@@ -158,77 +170,79 @@ def tile_picked_decorr_none_po_kernel(
         nc.vector.tensor_copy(rows_s[:, cols(1, D)].bitcast(I32), picked_s[:, cols(1, D)].bitcast(I32))
         for q in range(4):
             nc.sync.dma_start(
-                plane_s[32 * q : 32 * q + 4, :].bitcast(I32), rows_s[P - 16 + 4 * q : P - 12 + 4 * q, :].bitcast(I32)
+                plane_s[32 * q : 32 * q + 4, :].bitcast(I32),
+                rows_s[ROWS16 + 4 * q : ROWS16 + 4 * q + 4, :].bitcast(I32),
             )
-        wb_raw = placed("wb_raw", [P, 4, D], F32, 0)
+        wb_raw = in_turn("wb_raw", [P, 4, D], F32)
         load_rows(wb_raw, wb)
         nc.vector.tensor_copy(
             a_w[:].rearrange("p (t u r) -> p u t r", t=4, r=4), xw[:].bitcast(U32).indirect(offs_t[:])
         )
         q_w = [sbuf("q_w0", [P, H], U32)]
-        nc.vector.tensor_copy(q_w[0][:], xw[:].bitcast(U32).indirect(qs_t[:, cols(0, 16)]))
+        nc.vector.tensor_copy(q_w[0][:], xw[:].bitcast(U32).indirect(qs_t[:, cols(0, H // 16)]))
         deal(w1w_d[:], w1w[:])
 
         def x_tile(t):
             return a_w[:, cols(t)].bitcast(FP8X4), plane_s[:, cols(t)]
 
         def w1_tile(t):
-            return w1w_d[:, cols(t, H)].bitcast(FP4X4), plane_s[:, cols(8 + t)]
+            return w1w_d[:, cols(t, 2 * P)].bitcast(FP4X4), plane_s[:, 2 * D + P * t : 2 * D + P * t + P]
 
         def q_half(h):
-            return q_w[h][:], plane_s[:, cols(2 + h, H)]
+            return q_w[h][:], plane_s[:, D + H * h : D + H * h + H]
 
-        def round_wa(h, cast, slot=None):
-            dst = sbuf("wa_bf%d" % h, [P, H, 4], BF16, slot)
+        def round_wa(h, cast):
+            dst = sbuf("wa_bf%d" % h, [P, H, 4], BF16)
             cast(
                 dst[:].rearrange("p (t u r) j -> p t u j r", t=2, r=4),
                 wa_raw[:].rearrange("p j (u t r) -> p t u j r", t=4, r=4)[:, 2 * h : 2 * h + 2],
             )
             return dst
 
-        def round_wb(h, cast):
-            dst = sbuf("wb_bf1", [P, H, 4], BF16)[:] if h else z_wv[:, D - P : D + P]
-            cast(
+        def round_wb(h, dst):
+            nc.scalar.copy(
                 dst.rearrange("p (t m) j -> p m j t", t=2),
                 wb_raw[:].rearrange("p j (m t) -> p m j t", t=4)[:, :, :, 2 * h : 2 * h + 2],
             )
             return dst
 
-        warm = bank(3)
-        for r in range(2):
-            mm(warm[:], a_w[:, cols(r)].bitcast(FP8X4), rows_s[:, cols(r)], a_w[:].bitcast(FP8X4), rows_s[:, cols(0, D)])
+        warm_up(3)
         wa_bf = [round_wa(0, nc.vector.tensor_copy), round_wa(1, nc.scalar.copy)]
-        res_t = sbuf("res_t", [P, 4, D], F32, "wa_raw")
+        res_t = sbuf("res_t", [P, 4, D], F32, after="wa_raw")
         load_rows(res_t, res)
-        y_pl = [planes("y0", w1_tile, q_half(0), (4, 5, 6, 7), g_q)]
+        y_tiles = [gated_tiles("y0", w1_tile, q_half(0), (4, 5, 6, 7), g_q)]
         wa_q = [quantise("wa_q%d" % h, wa_bf[h]) for h in range(2)]
-        q_w.append(sbuf("q_w1", [P, H], U32, "wa_bf0"))
-        nc.vector.tensor_copy(q_w[1][:], xw[:].bitcast(U32).indirect(qs_t[:, cols(1, 16)]))
-        z_wv = sbuf("z_wv", [P, D + P, 4], BF16)
-        wb_bf = [round_wb(h, nc.scalar.copy) for h in range(2)]
+        q_w.append(sbuf("q_w1", [P, H], U32, after="wa_bf0"))
+        nc.vector.tensor_copy(q_w[1][:], xw[:].bitcast(U32).indirect(qs_t[:, cols(1, H // 16)]))
+        y0_wv = sbuf("y0_wv", [P, H + P, 4], BF16)
+        wb_bf = [round_wb(0, sbuf("wb_bf0", [P, H, 4], BF16)[:]), round_wb(1, y0_wv[:, P : P + H])]
         wb_q = [quantise("wb_q%d" % h, wb_bf[h]) for h in range(2)]
-        for t in range(4):
-            direct_bank(z_wv[:, cols(t)], t % 2, x_tile, whole(wa_q[t // 2]), t, g_t)
-        z2_pl = [planes("z2%d" % h, x_tile, whole(wb_q[h]), ((0, 1, 6, 7), (4, 5))[h], g_i[h]) for h in range(2)]
-        z4_wv = sbuf("z40_wv", [P, H, 4], BF16)
-        nc.gpsimd.tensor_scalar(z4_wv[:], y_pl[0][:].rearrange("p t n -> p n t"), 1.0, 0.0, MULT, ADD)
-        z_q = [quantise("z_q0", z_wv[:, cols(0, H)], offset=8 * H)]
-        z2_wv = weave("z20", z2_pl[0])
-        z_q.append(quantise("z_q1", z_wv[:, cols(1, H)], "g_i0"))
-        z2_q = [quantise("z2_q0", z2_wv)]
-        z2_wv = weave("z21", z2_pl[1])
-        z4_q = [quantise("z4_q0", z4_wv, "g_i1")]
-        z2_q.append(quantise("z2_q1", z2_wv))
-        y_pl.append(planes("y1", w1_tile, q_half(1), (6, 7), g_q))
-        c_pl = [planes("c%d" % h, tiles_of(z_q), whole(z2_q[h]), (6 * h, 6 * h + 1), g_k[h]) for h in range(2)]
-        warm = bank(1)
-        for r in range(2):
-            mm(warm[:], a_w[:, cols(r)].bitcast(FP8X4), rows_s[:, cols(r)], a_w[:].bitcast(FP8X4), rows_s[:, cols(0, D)])
-        z4_wv = weave("z41", y_pl[1])
-        z3_wv = weave("z30", c_pl[0])
-        z4_q.append(quantise("z4_q1", z4_wv, "g_k0"))
-        z3_q = [quantise("z3_q0", z3_wv)]
-        z3_wv = weave("z31", c_pl[1])
+        z_wv = [sbuf("z_wv0", [P, H, 4], BF16), in_turn("z_wv1", [P, H, 4], BF16)]
+        for h in range(2):
+            for u in range(2):
+                gated_woven(z_wv[h][:, cols(u)], u, x_tile, whole(wa_q[h]), u, g_t)
+        z2_banks = ((2, 3, 6, 7), (4, 5))
+        z2_tiles = [gated_tiles("z2%d" % h, x_tile, whole(wb_q[h]), z2_banks[h], g_i[h]) for h in range(2)]
+        for u in range(2):
+            nc.gpsimd.tensor_scalar(
+                y0_wv[:, cols(u)], y_tiles[0][:, :, cols(u)].rearrange("p t n -> p n t"), 1.0, 0.0, MULT, ADD
+            )
+        z_q = [quantise("z_q0", z_wv[0], after="wb_bf0")]
+        z2_wv = [weave("z20", z2_tiles[0])]
+        z_q.append(quantise("z_q1", z_wv[1], after="g_i0"))
+        z2_q = [quantise("z2_q0", z2_wv[0])]
+        z2_wv.append(weave("z21", z2_tiles[1]))
+        z4_q = [quantise("z4_q0", y0_wv[:, 0:H], after="g_i1")]
+        z2_q.append(quantise("z2_q1", z2_wv[1]))
+        y_tiles.append(gated_tiles("y1", w1_tile, q_half(1), (6, 7), g_q))
+        z3_banks = ((0, 1), (6, 7))
+        z3_tiles = [gated_tiles("c%d" % h, tiles_of(z_q), whole(z2_q[h]), z3_banks[h], g_k[h]) for h in range(2)]
+        warm_up(1)
+        y1_wv = weave("z41", y_tiles[1])
+        z3_wv = [weave("z30", z3_tiles[0])]
+        z4_q.append(quantise("z4_q1", y1_wv, after="g_k0"))
+        z3_q = [quantise("z3_q0", z3_wv[0])]
+        z3_wv.append(weave("z31", z3_tiles[1]))
 
         out_v = out_0.rearrange("(p t) v -> p t v", t=4)
         words_v = out_1[0].rearrange("p n t -> p (n t)").bitcast(I32)
@@ -236,28 +250,28 @@ def tile_picked_decorr_none_po_kernel(
         o_w = sbuf("o_w", [P, D], U32)
         o_f = sbuf("o_f", [P, 4, D], F32)
         o_bf = [sbuf("o_bf%d" % h, [P, H, 4], BF16) for h in range(2)]
-        z3_q.append(quantise("z3_q1", z3_wv))
-        accs = [bank(2 + t) for t in range(2)]
+        z3_q.append(quantise("z3_q1", z3_wv[1]))
+
+        def last_product(out, t, h):
+            lw, ls = tiles_of(z3_q)(t)
+            mm(out, lw, ls, z4_q[h][0][:].bitcast(FP8X4), z4_q[h][1][:])
+
+        first_pair = [bank(2 + t) for t in range(2)]
         for t in range(2):
             for h in range(2):
-                lw, ls = tiles_of(z3_q)(t)
-                mm(accs[t][:, cols(h, H)], lw, ls, z4_q[h][0][:].bitcast(FP8X4), z4_q[h][1][:])
-        for t in range(2):
-            acc = accs[t]
-            if t:
-                nc.vector.scalar_tensor_tensor(o_f[:, t], acc[:], -0.03125, res_t[:, t], MULT, ADD)
-            else:
-                scaled = sbuf("scaled", [P, D], F32)
-                nc.scalar.activation(scaled[:], acc[:], COPY, scale=-0.03125)
-                nc.gpsimd.tensor_tensor(o_f[:, t], scaled[:], res_t[:, t], ADD)
-            nc.sync.dma_start(out_v[:, t], o_f[:, t])
+                last_product(first_pair[t][:, cols(h, H)], t, h)
+        scaled = sbuf("scaled", [P, D], F32)
+        nc.scalar.activation(scaled[:], first_pair[0][:], COPY, scale=OUT_FACTOR)
+        nc.gpsimd.tensor_tensor(o_f[:, 0], scaled[:], res_t[:, 0], ADD)
+        nc.sync.dma_start(out_v[:, 0], o_f[:, 0])
+        nc.vector.scalar_tensor_tensor(o_f[:, 1], first_pair[1][:], OUT_FACTOR, res_t[:, 1], MULT, ADD)
+        nc.sync.dma_start(out_v[:, 1], o_f[:, 1])
         for h in range(2):
             acc = bank(4 + h)
             for e in range(2):
-                lw, ls = tiles_of(z3_q)(2 + e)
-                mm(acc[:, cols(e, H)], lw, ls, z4_q[h][0][:].bitcast(FP8X4), z4_q[h][1][:])
+                last_product(acc[:, cols(e, H)], 2 + e, h)
             nc.vector.scalar_tensor_tensor(
-                o_f[:, 2:4, cols(h, H)], acc[:].rearrange("p (e n) -> p e n", e=2), -0.03125,
+                o_f[:, 2:4, cols(h, H)], acc[:].rearrange("p (e n) -> p e n", e=2), OUT_FACTOR,
                 res_t[:, 2:4, cols(h, H)], MULT, ADD,
             )
             nc.sync.dma_start(out_v[:, 2:4, cols(h, H)], o_f[:, 2:4, cols(h, H)])

@@ -257,16 +257,15 @@ def tile_picked_decorr_none_po_kernel(
             mm(out, lw, ls, z4_q[h][0][:].bitcast(FP8X4), z4_q[h][1][:])
 
         first_pair = [bank(2 + t) for t in range(2)]
-        for t in range(2):
+        for t in (1, 0):
             for h in range(2):
                 last_product(first_pair[t][:, cols(h, H)], t, h)
         scaled = sbuf("scaled", [P, D], F32)
-        nc.scalar.activation(scaled[:], first_pair[0][:], COPY, scale=OUT_FACTOR)
-        nc.gpsimd.tensor_tensor(o_f[:, 0], scaled[:], res_t[:, 0], ADD)
+        nc.scalar.activation(scaled[:], first_pair[1][:], COPY, scale=OUT_FACTOR)
+        nc.vector.scalar_tensor_tensor(o_f[:, 0], first_pair[0][:], OUT_FACTOR, res_t[:, 0], MULT, ADD)
         nc.sync.dma_start(out_v[:, 0], o_f[:, 0])
-        nc.vector.scalar_tensor_tensor(o_f[:, 1], first_pair[1][:], OUT_FACTOR, res_t[:, 1], MULT, ADD)
-        nc.sync.dma_start(out_v[:, 1], o_f[:, 1])
         for h in range(2):
+            nc.gpsimd.tensor_tensor(o_f[:, 1, cols(h, H)], scaled[:, cols(h, H)], res_t[:, 1, cols(h, H)], ADD)
             acc = bank(4 + h)
             for e in range(2):
                 last_product(acc[:, cols(e, H)], 2 + e, h)
@@ -274,7 +273,7 @@ def tile_picked_decorr_none_po_kernel(
                 o_f[:, 2:4, cols(h, H)], acc[:].rearrange("p (e n) -> p e n", e=2), OUT_FACTOR,
                 res_t[:, 2:4, cols(h, H)], MULT, ADD,
             )
-            nc.sync.dma_start(out_v[:, 2:4, cols(h, H)], o_f[:, 2:4, cols(h, H)])
+            nc.sync.dma_start(out_v[:, 1:4, cols(h, H)], o_f[:, 1:4, cols(h, H)])
         for c in range(4):
             cast = nc.vector.tensor_copy if c % 2 else nc.scalar.copy
             cast(

@@ -262,10 +262,10 @@ def tile_picked_decorr_none_po_kernel(
                 last_product(first_pair[t][:, cols(h, H)], t, h)
         scaled = sbuf("scaled", [P, D], F32)
         nc.scalar.activation(scaled[:], first_pair[1][:], COPY, scale=OUT_FACTOR)
+        nc.gpsimd.tensor_tensor(o_f[:, 1], scaled[:], res_t[:, 1], ADD)
         nc.vector.scalar_tensor_tensor(o_f[:, 0], first_pair[0][:], OUT_FACTOR, res_t[:, 0], MULT, ADD)
         nc.sync.dma_start(out_v[:, 0], o_f[:, 0])
         for h in range(2):
-            nc.gpsimd.tensor_tensor(o_f[:, 1, cols(h, H)], scaled[:, cols(h, H)], res_t[:, 1, cols(h, H)], ADD)
             acc = bank(4 + h)
             for e in range(2):
                 last_product(acc[:, cols(e, H)], 2 + e, h)

@@ -168,11 +168,8 @@ def tile_picked_decorr_none_po_kernel(
         deal(rows_s[:, cols(0, D)], picked_s[:, 0:D])
         deal(rows_s[:, cols(2, D)], w1s[:])
         nc.vector.tensor_copy(rows_s[:, cols(1, D)].bitcast(I32), picked_s[:, cols(1, D)].bitcast(I32))
-        for q in range(4):
-            nc.sync.dma_start(
-                plane_s[32 * q : 32 * q + 4, :].bitcast(I32),
-                rows_s[ROWS16 + 4 * q : ROWS16 + 4 * q + 4, :].bitcast(I32),
-            )
+        for r in range(4):
+            nc.sync.dma_start(plane_s[r:P:32, :].bitcast(I32), rows_s[ROWS16 + r : P : 4, :].bitcast(I32))
         wb_raw = in_turn("wb_raw", [P, 4, D], F32)
         load_rows(wb_raw, wb)
         nc.vector.tensor_copy(
@@ -206,7 +203,6 @@ def tile_picked_decorr_none_po_kernel(
             )
             return dst
 
-        warm_up(3)
         wa_bf = [round_wa(0, nc.vector.tensor_copy), round_wa(1, nc.scalar.copy)]
         res_t = sbuf("res_t", [P, 4, D], F32, after="wa_raw")
         load_rows(res_t, res)
@@ -283,6 +279,6 @@ def tile_picked_decorr_none_po_kernel(
         for h in range(2):
             nc.vector.quantize_mx(out=o_w[:, cols(h, H)].bitcast(FP8X4), scales=o_s[:, cols(h, H)], in_=flat(o_bf[h][:]))
             nc.sync.dma_start(words_v[:, cols(h, H)], o_w[:, cols(h, H)].bitcast(I32))
-        for q in range(4):
-            eng = nc.scalar if q % 2 else nc.sync
-            eng.dma_start(out_2[0, 4 * q : 4 * q + 4, :].bitcast(I32), o_s[32 * q : 32 * q + 4, :].bitcast(I32))
+        for r in range(4):
+            eng = nc.scalar if r % 2 else nc.sync
+            eng.dma_start(out_2[0, r:16:4, :].bitcast(I32), o_s[r:P:32, :].bitcast(I32))

@@ -24,6 +24,7 @@ ROWS4 = P - 4
 QUAD3 = 96
 WARM_PASSES = 2
 OUT_FACTOR = -0.03125
+VECTOR_RUNS = 24
 FLOPS = 5 * 2 * D * D * D
 
 
@@ -62,8 +63,8 @@ def tile_picked_decorr_none_po_kernel(
         plane_s = sbuf("plane_s", [P, 3 * D], U8)
 
         nc.gpsimd.memset(xs[0:ROWS16, :].bitcast(I32), 0)
+        nc.vector.memset(gate_rows[0:ROWS4, :], 0.0)
         nc.vector.memset(w1s[0:ROWS16, :].bitcast(I32), 0)
-        nc.vector.memset(gate_rows[QUAD3:ROWS4, :], 0.0)
         nc.vector.memset(plane_s[:].bitcast(I32), 0)
         make_identity(nc, ident[:])
 
@@ -81,9 +82,7 @@ def tile_picked_decorr_none_po_kernel(
         nc.sync.dma_start(w1w[:].bitcast(I32), w1_words[0].bitcast(I32))
 
         gate_dealt = sbuf("gate_dealt", [P, 4, P], F32)
-        nc.scalar.activation(
-            gate_dealt[0:QUAD3], ident[0:QUAD3].unsqueeze(1).to_broadcast([QUAD3, 4, P]), COPY, scale=0.0
-        )
+        nc.scalar.activation(gate_dealt[0:QUAD3].rearrange("g t c -> g (t c)"), gate_rows[0:QUAD3], COPY)
         nc.scalar.copy(
             gate_dealt[QUAD3:P].rearrange("g t (u r) -> g t u r", r=4),
             gate_rows[QUAD3:P].rearrange("g (u t r) -> g t u r", t=4, r=4),
@@ -150,10 +149,10 @@ def tile_picked_decorr_none_po_kernel(
         def tiles_of(q):
             return lambda t: (q[t // 2][0][:, cols(t % 2)].bitcast(FP8X4), q[t // 2][1][:, cols(t % 2)])
 
-        def deal(dst, src):
-            nc.vector.tensor_copy(
-                dst.bitcast(I32).rearrange("p (t u w) -> p t u w", t=4, u=32),
-                src.bitcast(I32).rearrange("p (u t w) -> p t u w", t=4, u=32),
+        def deal(move, word, dst, src):
+            move(
+                dst.bitcast(word).rearrange("p (t u w) -> p t u w", t=4, u=32),
+                src.bitcast(word).rearrange("p (u t w) -> p t u w", t=4, u=32),
             )
 
         def warm_up(b):
@@ -165,8 +164,8 @@ def tile_picked_decorr_none_po_kernel(
         w1w_d = sbuf("w1w_d", [P, 2 * D], U8)
         nc.vector.tensor_copy(picked_s[:, 0:D], xs[:].indirect(offs_t[:]))
         nc.vector.tensor_copy(picked_s[:, D : 2 * D], xs[:].indirect(qs_t[:]))
-        deal(rows_s[:, cols(0, D)], picked_s[:, 0:D])
-        deal(rows_s[:, cols(2, D)], w1s[:])
+        deal(nc.scalar.copy, U32, rows_s[:, cols(2, D)], w1s[:])
+        deal(nc.vector.tensor_copy, I32, rows_s[:, cols(0, D)], picked_s[:, 0:D])
         nc.vector.tensor_copy(rows_s[:, cols(1, D)].bitcast(I32), picked_s[:, cols(1, D)].bitcast(I32))
         for r in range(4):
             nc.sync.dma_start(plane_s[r:P:32, :].bitcast(I32), rows_s[ROWS16 + r : P : 4, :].bitcast(I32))
@@ -177,7 +176,7 @@ def tile_picked_decorr_none_po_kernel(
         )
         q_w = [sbuf("q_w0", [P, H], U32)]
         nc.vector.tensor_copy(q_w[0][:], xw[:].bitcast(U32).indirect(qs_t[:, cols(0, H // 16)]))
-        deal(w1w_d[:], w1w[:])
+        deal(nc.vector.tensor_copy, I32, w1w_d[:], w1w[:])
 
         def x_tile(t):
             return a_w[:, cols(t)].bitcast(FP8X4), plane_s[:, cols(t)]
@@ -188,13 +187,11 @@ def tile_picked_decorr_none_po_kernel(
         def q_half(h):
             return q_w[h][:], plane_s[:, D + H * h : D + H * h + H]
 
-        def round_wa(h, cast):
-            dst = sbuf("wa_bf%d" % h, [P, H, 4], BF16)
+        def round_wa(cast, h, first, last):
             cast(
-                dst[:].rearrange("p (t u r) j -> p t u j r", t=2, r=4),
-                wa_raw[:].rearrange("p j (u t r) -> p t u j r", t=4, r=4)[:, 2 * h : 2 * h + 2],
+                wa_bf[h][:].rearrange("p (t u r) j -> p t u j r", t=2, r=4)[:, :, first:last],
+                wa_raw[:].rearrange("p j (u t r) -> p t u j r", t=4, r=4)[:, 2 * h : 2 * h + 2, first:last],
             )
-            return dst
 
         def round_wb(h, dst):
             nc.scalar.copy(
@@ -203,7 +200,10 @@ def tile_picked_decorr_none_po_kernel(
             )
             return dst
 
-        wa_bf = [round_wa(0, nc.vector.tensor_copy), round_wa(1, nc.scalar.copy)]
+        wa_bf = [sbuf("wa_bf%d" % h, [P, H, 4], BF16) for h in range(2)]
+        round_wa(nc.vector.tensor_copy, 0, 0, VECTOR_RUNS)
+        round_wa(nc.scalar.copy, 0, VECTOR_RUNS, 32)
+        round_wa(nc.scalar.copy, 1, 0, 32)
         res_t = sbuf("res_t", [P, 4, D], F32, after="wa_raw")
         load_rows(res_t, res)
         y_tiles = [gated_tiles("y0", w1_tile, q_half(0), (4, 5, 6, 7), g_q)]

@@ -22,7 +22,6 @@ T = 2048
 ROWS16 = P - 16
 ROWS4 = P - 4
 QUAD3 = 96
-WARM_PASSES = 2
 OUT_FACTOR = -0.03125
 VECTOR_RUNS = 24
 FLOPS = 5 * 2 * D * D * D
@@ -155,11 +154,6 @@ def tile_picked_decorr_none_po_kernel(
                 src.bitcast(word).rearrange("p (u t w) -> p t u w", t=4, u=32),
             )
 
-        def warm_up(b):
-            acc = bank(b)
-            for r in range(WARM_PASSES):
-                mm(acc[:], a_w[:, cols(r)].bitcast(FP8X4), rows_s[:, cols(r)], a_w[:].bitcast(FP8X4), rows_s[:, cols(0, D)])
-
         a_w = sbuf("a_w", [P, D], U32)
         w1w_d = sbuf("w1w_d", [P, 2 * D], U8)
         nc.vector.tensor_copy(picked_s[:, 0:D], xs[:].indirect(offs_t[:]))
@@ -233,7 +227,6 @@ def tile_picked_decorr_none_po_kernel(
         y_tiles.append(gated_tiles("y1", w1_tile, q_half(1), (6, 7), g_q))
         z3_banks = ((0, 1), (6, 7))
         z3_tiles = [gated_tiles("c%d" % h, tiles_of(z_q), whole(z2_q[h]), z3_banks[h], g_k[h]) for h in range(2)]
-        warm_up(1)
         y1_wv = weave("z41", y_tiles[1])
         z3_wv = [weave("z30", z3_tiles[0])]
         z4_q.append(quantise("z4_q1", y1_wv, after="g_k0"))

from contextlib import ExitStack

import concourse.mybir as mybir
from concourse.masks import make_identity

F32 = mybir.dt.float32
BF16 = mybir.dt.bfloat16
I32 = mybir.dt.int32
U32 = mybir.dt.uint32
U16 = mybir.dt.uint16
U8 = mybir.dt.uint8
FP8X4 = mybir.dt.float8_e4m3fn_x4
FP4X4 = mybir.dt.float4_e2m1fn_x4
MULT = mybir.AluOpType.mult
ADD = mybir.AluOpType.add
COPY = mybir.ActivationFunctionType.Copy

P = 128
D = 512
H = 256
T = 2048
ROWS16 = P - 16
ROWS4 = P - 4
QUAD3 = 96
OUT_FACTOR = -0.03125
VECTOR_RUNS = 24
FLOPS = 5 * 2 * D * D * D


def tile_picked_decorr_none_po_kernel(
    tc, x_words, x_scales, wa, wb, gt, gi, w1_words, w1_scales, gk, gq, res, offs, qs, out_0, out_1, out_2
):
    nc = tc.nc
    with ExitStack() as ctx:
        sb = ctx.enter_context(tc.tile_pool(name="sb", bufs=1))
        shared = ctx.enter_context(tc.tile_pool(name="shared", bufs=1))
        ps = ctx.enter_context(tc.psum_pool(name="ps", bufs=1))

        def sbuf(name, shape, dtype, after=None):
            return sb.tile(shape, dtype, name=name, tag=after or name, align_bytes=64)

        def in_turn(name, shape, dtype):
            return shared.tile(shape, dtype, name=name, align_bytes=64, offset=0)

        def bank(b):
            return ps.tile([P, D], F32, name="bank%d" % b)

        def cols(t, n=P):
            return slice(n * t, n * t + n)

        offs_t = sbuf("offs_t", [P, D // 16], U16)
        qs_t = sbuf("qs_t", [P, D // 16], U16)
        xw = sbuf("xw", [P, T], I32)
        xs = sbuf("xs", [P, T], U8)
        wa_raw = sbuf("wa_raw", [P, 4, D], F32)
        w1w = sbuf("w1w", [P, 2 * D], U8)
        gate_rows = sbuf("gate_rows", [P, D], F32)
        ident = sbuf("ident", [P, P], F32)
        picked_s = in_turn("picked_s", [P, 2 * D], U8)
        w1s = sbuf("w1s", [P, D], U8)
        rows_s = sbuf("rows_s", [P, 3 * D], U8)
        plane_s = sbuf("plane_s", [P, 3 * D], U8)

        nc.gpsimd.memset(xs[0:ROWS16, :].bitcast(I32), 0)
        nc.vector.memset(gate_rows[0:ROWS4, :], 0.0)
        nc.vector.memset(w1s[0:ROWS16, :].bitcast(I32), 0)
        nc.vector.memset(plane_s[:].bitcast(I32), 0)
        make_identity(nc, ident[:])

        def load_rows(dst, w):
            nc.sync.dma_start(dst[:], w.rearrange("(p j) c -> p j c", j=4))

        nc.sync.dma_start(offs_t[:], offs)
        nc.sync.dma_start(qs_t[:], qs)
        nc.sync.dma_start(xs[ROWS16:P, :].bitcast(I32), x_scales[0].bitcast(I32))
        nc.sync.dma_start(w1s[ROWS16:P, :].bitcast(I32), w1_scales[0].bitcast(I32))
        nc.sync.dma_start(xw[:], x_words[0].rearrange("p n t -> p (n t)").bitcast(I32))
        for g, vector in enumerate((gt, gi, gq, gk)):
            nc.sync.dma_start(gate_rows[ROWS4 + g : ROWS4 + g + 1, :], vector.rearrange("n o -> o n"))
        load_rows(wa_raw, wa)
        nc.sync.dma_start(w1w[:].bitcast(I32), w1_words[0].bitcast(I32))

        gate_dealt = sbuf("gate_dealt", [P, 4, P], F32)
        nc.scalar.activation(gate_dealt[0:QUAD3].rearrange("g t c -> g (t c)"), gate_rows[0:QUAD3], COPY)
        nc.scalar.copy(
            gate_dealt[QUAD3:P].rearrange("g t (u r) -> g t u r", r=4),
            gate_rows[QUAD3:P].rearrange("g (u t r) -> g t u r", t=4, r=4),
        )
        gate_ps = bank(7)
        for t in range(4):
            nc.tensor.transpose(gate_ps[:, cols(t)], gate_dealt[:, t], ident[:])
        turned = gate_ps[:].rearrange("p (t g) -> p g t", t=4)

        def gate_tile(name, g, factor=1.0):
            tile = sbuf(name, [P, 4], F32)
            nc.scalar.activation(tile[:], turned[:, ROWS4 + g], COPY, scale=factor)
            return tile[:]

        g_t, g_q = gate_tile("g_t", 0), gate_tile("g_q", 2)
        g_i = [gate_tile("g_i%d" % h, 1) for h in range(2)]
        g_k = [gate_tile("g_k%d" % h, 3, 0.0625) for h in range(2)]

        def flat(ap):
            return ap.rearrange("p n t -> p (n t)")

        def quantise(name, woven, after=None):
            codes = sbuf(name + "_c", [P, H], U32, after)
            scales = sbuf(name + "_s", [P, H], U8)
            nc.vector.quantize_mx(out=codes[:].bitcast(FP8X4), scales=scales[:], in_=flat(woven[:]))
            return codes, scales

        def mm(out, lw, ls, rw, rs):
            nc.tensor.matmul_mx(out=out, lhsT=lw, lhsT_scale=ls, rhs=rw, rhs_scale=rs, start=True, stop=True)

        def gated_tiles(name, stationary, moving, banks, gate):
            tiles = sbuf(name + "_pl", [P, 4, H], BF16)
            per_bank = 4 // len(banks)
            for u, b in enumerate(banks):
                acc = bank(b)
                places = range(per_bank * u, per_bank * (u + 1))
                for t in places:
                    lw, ls = stationary(t)
                    mm(acc[:, cols(t % per_bank, H)], lw, ls, moving[0].bitcast(FP8X4), moving[1])
                for t in places:
                    nc.scalar.activation(tiles[:, t, :], acc[:, cols(t % per_bank, H)], COPY, scale=gate[:, t : t + 1])
            return tiles

        def weave(name, tiles):
            woven = sbuf(name + "_wv", [P, H, 4], BF16)
            nc.vector.tensor_copy(
                woven[:].rearrange("p (c i) t -> p c t i", i=4), tiles[:].rearrange("p t (c i) -> p c t i", i=4)
            )
            return woven

        def gated_woven(dst, u, stationary, moving, b, gate):
            acc = bank(b)
            for t in range(4):
                lw, ls = stationary(t)
                mm(acc[:, cols(t)], lw, ls, moving[0][:, cols(u)].bitcast(FP8X4), moving[1][:, cols(u)])
            nc.vector.tensor_tensor(
                dst.rearrange("p (c i) t -> p c t i", i=2), acc[:].rearrange("p (t c i) -> p c t i", t=4, i=2),
                gate.unsqueeze(1).unsqueeze(3).to_broadcast([P, P // 2, 4, 2]), MULT,
            )

        def whole(q):
            return q[0][:], q[1][:]

        def tiles_of(q):
            return lambda t: (q[t // 2][0][:, cols(t % 2)].bitcast(FP8X4), q[t // 2][1][:, cols(t % 2)])

        def deal(move, word, dst, src):
            move(
                dst.bitcast(word).rearrange("p (t u w) -> p t u w", t=4, u=32),
                src.bitcast(word).rearrange("p (u t w) -> p t u w", t=4, u=32),
            )

        a_w = sbuf("a_w", [P, D], U32)
        w1w_d = sbuf("w1w_d", [P, 2 * D], U8)
        nc.vector.tensor_copy(picked_s[:, 0:D], xs[:].indirect(offs_t[:]))
        nc.vector.tensor_copy(picked_s[:, D : 2 * D], xs[:].indirect(qs_t[:]))
        deal(nc.scalar.copy, U32, rows_s[:, cols(2, D)], w1s[:])
        deal(nc.vector.tensor_copy, I32, rows_s[:, cols(0, D)], picked_s[:, 0:D])
        nc.vector.tensor_copy(rows_s[:, cols(1, D)].bitcast(I32), picked_s[:, cols(1, D)].bitcast(I32))
        for r in range(4):
            nc.sync.dma_start(plane_s[r:P:32, :].bitcast(I32), rows_s[ROWS16 + r : P : 4, :].bitcast(I32))
        wb_raw = in_turn("wb_raw", [P, 4, D], F32)
        load_rows(wb_raw, wb)
        nc.vector.tensor_copy(
            a_w[:].rearrange("p (t u r) -> p u t r", t=4, r=4), xw[:].bitcast(U32).indirect(offs_t[:])
        )
        q_w = [sbuf("q_w0", [P, H], U32)]
        nc.vector.tensor_copy(q_w[0][:], xw[:].bitcast(U32).indirect(qs_t[:, cols(0, H // 16)]))
        deal(nc.vector.tensor_copy, I32, w1w_d[:], w1w[:])

        def x_tile(t):
            return a_w[:, cols(t)].bitcast(FP8X4), plane_s[:, cols(t)]

        def w1_tile(t):
            return w1w_d[:, cols(t, 2 * P)].bitcast(FP4X4), plane_s[:, 2 * D + P * t : 2 * D + P * t + P]

        def q_half(h):
            return q_w[h][:], plane_s[:, D + H * h : D + H * h + H]

        def round_wa(cast, h, first, last):
            cast(
                wa_bf[h][:].rearrange("p (t u r) j -> p t u j r", t=2, r=4)[:, :, first:last],
                wa_raw[:].rearrange("p j (u t r) -> p t u j r", t=4, r=4)[:, 2 * h : 2 * h + 2, first:last],
            )

        def round_wb(h, dst):
            nc.scalar.copy(
                dst.rearrange("p (t m) j -> p m j t", t=2),
                wb_raw[:].rearrange("p j (m t) -> p m j t", t=4)[:, :, :, 2 * h : 2 * h + 2],
            )
            return dst

        wa_bf = [sbuf("wa_bf%d" % h, [P, H, 4], BF16) for h in range(2)]
        round_wa(nc.vector.tensor_copy, 0, 0, VECTOR_RUNS)
        round_wa(nc.scalar.copy, 0, VECTOR_RUNS, 32)
        round_wa(nc.scalar.copy, 1, 0, 32)
        res_t = sbuf("res_t", [P, 4, D], F32, after="wa_raw")
        load_rows(res_t, res)
        y_tiles = [gated_tiles("y0", w1_tile, q_half(0), (4, 5, 6, 7), g_q)]
        wa_q = [quantise("wa_q%d" % h, wa_bf[h]) for h in range(2)]
        q_w.append(sbuf("q_w1", [P, H], U32, after="wa_bf0"))
        nc.vector.tensor_copy(q_w[1][:], xw[:].bitcast(U32).indirect(qs_t[:, cols(1, H // 16)]))
        y0_wv = sbuf("y0_wv", [P, H + P, 4], BF16)
        wb_bf = [round_wb(0, sbuf("wb_bf0", [P, H, 4], BF16)[:]), round_wb(1, y0_wv[:, P : P + H])]
        wb_q = [quantise("wb_q%d" % h, wb_bf[h]) for h in range(2)]
        z_wv = [sbuf("z_wv0", [P, H, 4], BF16), in_turn("z_wv1", [P, H, 4], BF16)]
        for h in range(2):
            for u in range(2):
                gated_woven(z_wv[h][:, cols(u)], u, x_tile, whole(wa_q[h]), u, g_t)
        z2_banks = ((2, 3, 6, 7), (4, 5))
        z2_tiles = [gated_tiles("z2%d" % h, x_tile, whole(wb_q[h]), z2_banks[h], g_i[h]) for h in range(2)]
        for u in range(2):
            nc.gpsimd.tensor_scalar(
                y0_wv[:, cols(u)], y_tiles[0][:, :, cols(u)].rearrange("p t n -> p n t"), 1.0, 0.0, MULT, ADD
            )
        z_q = [quantise("z_q0", z_wv[0], after="wb_bf0")]
        z2_wv = [weave("z20", z2_tiles[0])]
        z_q.append(quantise("z_q1", z_wv[1], after="g_i0"))
        z2_q = [quantise("z2_q0", z2_wv[0])]
        z2_wv.append(weave("z21", z2_tiles[1]))
        z4_q = [quantise("z4_q0", y0_wv[:, 0:H], after="g_i1")]
        z2_q.append(quantise("z2_q1", z2_wv[1]))
        y_tiles.append(gated_tiles("y1", w1_tile, q_half(1), (6, 7), g_q))
        z3_banks = ((0, 1), (6, 7))
        z3_tiles = [gated_tiles("c%d" % h, tiles_of(z_q), whole(z2_q[h]), z3_banks[h], g_k[h]) for h in range(2)]
        y1_wv = weave("z41", y_tiles[1])
        z3_wv = [weave("z30", z3_tiles[0])]
        z4_q.append(quantise("z4_q1", y1_wv, after="g_k0"))
        z3_q = [quantise("z3_q0", z3_wv[0])]
        z3_wv.append(weave("z31", z3_tiles[1]))

        out_v = out_0.rearrange("(p t) v -> p t v", t=4)
        words_v = out_1[0].rearrange("p n t -> p (n t)").bitcast(I32)
        o_s = sbuf("o_s", [P, D], U8)
        o_w = sbuf("o_w", [P, D], U32)
        o_f = sbuf("o_f", [P, 4, D], F32)
        o_bf = [sbuf("o_bf%d" % h, [P, H, 4], BF16) for h in range(2)]
        z3_q.append(quantise("z3_q1", z3_wv[1]))

        def last_product(out, t, h):
            lw, ls = tiles_of(z3_q)(t)
            mm(out, lw, ls, z4_q[h][0][:].bitcast(FP8X4), z4_q[h][1][:])

        first_pair = [bank(2 + t) for t in range(2)]
        for t in (1, 0):
            for h in range(2):
                last_product(first_pair[t][:, cols(h, H)], t, h)
        scaled = sbuf("scaled", [P, D], F32)
        nc.scalar.activation(scaled[:], first_pair[1][:], COPY, scale=OUT_FACTOR)
        nc.gpsimd.tensor_tensor(o_f[:, 1], scaled[:], res_t[:, 1], ADD)
        nc.vector.scalar_tensor_tensor(o_f[:, 0], first_pair[0][:], OUT_FACTOR, res_t[:, 0], MULT, ADD)
        nc.sync.dma_start(out_v[:, 0], o_f[:, 0])
        for h in range(2):
            acc = bank(4 + h)
            for e in range(2):
                last_product(acc[:, cols(e, H)], 2 + e, h)
            nc.vector.scalar_tensor_tensor(
                o_f[:, 2:4, cols(h, H)], acc[:].rearrange("p (e n) -> p e n", e=2), OUT_FACTOR,
                res_t[:, 2:4, cols(h, H)], MULT, ADD,
            )
            nc.sync.dma_start(out_v[:, 1:4, cols(h, H)], o_f[:, 1:4, cols(h, H)])
        for c in range(4):
            cast = nc.vector.tensor_copy if c % 2 else nc.scalar.copy
            cast(
                o_bf[c // 2][:, cols(c % 2)].rearrange("p (c i) t -> p c t i", i=4),
                o_f[:, :, cols(c)].rearrange("p t (c i) -> p c t i", i=4),
            )
        for h in range(2):
            nc.vector.quantize_mx(out=o_w[:, cols(h, H)].bitcast(FP8X4), scales=o_s[:, cols(h, H)], in_=flat(o_bf[h][:]))
            nc.sync.dma_start(words_v[:, cols(h, H)], o_w[:, cols(h, H)].bitcast(I32))
        for r in range(4):
            eng = nc.scalar if r % 2 else nc.sync
            eng.dma_start(out_2[0, r:16:4, :].bitcast(I32), o_s[r:P:32, :].bitcast(I32))
